import numpy as np
import ml_dtypes


def mxq(x, axis, fmt="e4m3"):
    dtype, down = {"e4m3": (ml_dtypes.float8_e4m3fn, 7), "e5m2": (ml_dtypes.float8_e5m2, 14)}[fmt]
    v = np.moveaxis(np.asarray(x, np.float32).astype(ml_dtypes.bfloat16).astype(np.float64), axis, -1)
    blocks = v.reshape(v.shape[:-1] + (-1, 32))
    amax = np.abs(blocks).max(-1, keepdims=True)
    byte = np.maximum(np.where(amax > 0, np.frexp(amax)[1] - 1 + 127, 0) - down, 1)
    scale = np.exp2(byte - 127.0)
    codes = (blocks / scale).astype(np.float32).astype(dtype).astype(np.float64)
    return np.moveaxis((codes * scale).reshape(v.shape), -1, axis)


WIDE = False


def mx_kscale(k):
    if not WIDE:
        return np.ones(k)
    levels = np.array([18, -18])
    if k % 512:
        return np.exp2(np.random.permutation(np.resize(levels, k // 32))).repeat(32)
    a = np.empty((k // 512, 16))
    for p in range(k // 512):
        a[p, :8] = np.random.permutation(np.resize(levels, 8))
        for g in range(8):
            far = levels[np.abs(levels - a[p, g]) >= 10]
            a[p, g + 8] = far[np.random.randint(len(far))]
    return np.exp2(a.ravel()).repeat(32)


def f64(x):
    return np.asarray(x).astype(np.float64)


def striped(idx):
    return np.tile(np.asarray(idx).reshape(-1, 16).T, (8, 1)).astype(np.uint16)


def unstriped(offs):
    return offs[:16].T.reshape(-1).astype(np.int64)

def planes(y):
    n, m = y.shape
    v = y.astype(np.float32).astype(ml_dtypes.bfloat16).astype(np.float64).reshape(n // 32, 32, m)
    top = np.abs(v).max(1)
    byte = np.clip(np.where(top > 0, np.frexp(top)[1] - 1 + 127 - 7, 1), 1, 254)
    codes = (v * np.exp2(127.0 - byte)[:, None, :]).reshape(n, m).astype(np.float32).astype(ml_dtypes.float8_e4m3fn).view(np.uint8)
    words = codes.reshape(n // 512, 128, 4, m).transpose(0, 1, 3, 2)
    return np.ascontiguousarray(words), np.ascontiguousarray(byte.astype(np.uint8).reshape(n // 512, 16, m))


def setup_inputs():
    n = np.random.standard_normal
    uni = np.random.uniform
    idx = np.random.permutation(2048)[:512]
    x_ = uni(0.5, 1.5, (512, 2048))
    f_d = mx_kscale(512)
    return {
        "Pc": (uni(0.5, 1.5, (512, 512)) / 512 * f_d[:, None]).astype(np.float32),
        "xT": (x_ / f_d[:, None]).astype(np.float32),
        "xE": (x_).astype(np.float32),
        "er": np.tile(n(2048), (128, 1)).astype(np.float32),
        "offs": striped(idx),
    }


def reference(Pc, xT, xE, er, offs):
    idx = unstriped(offs)
    a = f64(xT)[:, idx]
    b = f64(xE)[:, idx]
    er_i = f64(er)[:1][:, idx]
    k = mxq(f64(Pc), 0, "e4m3").T @ mxq(a, 0, "e4m3")
    q = b * k
    qt = q.T
    s = (qt).sum(-1, keepdims=True)
    sr = s.T
    up = k * er_i / (1.0 + sr)
    out_0 = np.zeros((512, 2048))
    out_0[:, idx] = up
    return (out_0,) + planes(out_0)

@@ -1,0 +1,180 @@
+from contextlib import ExitStack
+
+import concourse.mybir as mybir
+from concourse.masks import make_identity
+
+F32 = mybir.dt.float32
+BF16 = mybir.dt.bfloat16
+I32 = mybir.dt.int32
+U32 = mybir.dt.uint32
+U16 = mybir.dt.uint16
+U8 = mybir.dt.uint8
+FP8X4 = mybir.dt.float8_e4m3fn_x4
+MULT = mybir.AluOpType.mult
+COPY = mybir.ActivationFunctionType.Copy
+
+P = 128
+LANES = 4
+SLOTS = 512
+TABLE = 2048
+HALF = SLOTS // 2
+BLOCKS = SLOTS // P
+FLOPS = 2 * 512 * 512 * 512
+
+CHUNKS = (
+    (0, 512, "scalar", "scalar"),
+    (512, 512, "vector", "vector"),
+    (1024, 512, "vector", "vector"),
+    (1536, 256, "vector", "scalar"),
+    (1792, 256, "vector", "scalar"),
+)
+
+
+def copy_on(nc, engine, out, in_):
+    if engine == "scalar":
+        nc.scalar.copy(out=out, in_=in_)
+    else:
+        nc.vector.tensor_copy(out=out, in_=in_)
+
+
+def interleave(nc, engine, grouped, rows):
+    copy_on(nc, engine, grouped.rearrange("p (c i) t -> p c t i", i=4), rows.rearrange("p t (c i) -> p c t i", i=4))
+
+
+def tile_attend_grls_pl_kernel(tc, Pc, xT, xE, er, offs, out_0, out_1, out_2):
+    nc = tc.nc
+    with ExitStack() as ctx:
+        keep = ctx.enter_context(tc.tile_pool(name="keep", bufs=1))
+        psum = ctx.enter_context(tc.psum_pool(name="psum", bufs=1))
+
+        offsets = keep.tile([P, SLOTS // 16], U16, name="offsets")
+        nc.sync.dma_start(offsets[:], offs)
+        half_offsets = [offsets[:, h * HALF // 16 : (h + 1) * HALF // 16] for h in range(2)]
+
+        xT_rows = xT.rearrange("(p t) c -> p t c", t=LANES)
+        xE_rows = xE.rearrange("(p t) c -> p t c", t=LANES)
+        out_rows = out_0.rearrange("(p t) c -> p t c", t=LANES)
+
+        xT_sb = [keep.tile([P, TABLE], F32, name=f"xT{t}", tag=f"table{t}") for t in range(LANES)]
+        pc_sb = keep.tile([P, LANES, SLOTS], F32, name="pc_sb")
+        er_sb = keep.tile([P, TABLE], F32, name="er_sb")
+        windows = [keep.tile([P, TABLE], F32, name=f"window{t}") for t in range(LANES)]
+
+        for t in range(LANES):
+            nc.sync.dma_start(xT_sb[t][:], xT_rows[:, t, :])
+        nc.sync.dma_start(pc_sb[:], Pc.rearrange("(p j) e -> p j e", j=LANES))
+
+        nc.vector.memset(er_sb[:], 0.0)
+        nc.sync.dma_start(er_sb[0:1, :], er[0:1, :])
+        nc.vector.memset(windows[0][:], 0.0)
+        identity = keep.tile([P, P], F32, name="identity")
+        make_identity(nc, identity[:])
+        for t in range(1, LANES):
+            nc.gpsimd.memset(windows[t][:], 0.0)
+
+        x_listed = keep.tile([P, LANES, SLOTS], BF16, name="x_listed")
+        for t in range(LANES):
+            nc.vector.tensor_copy(out=x_listed[:, t, :], in_=xT_sb[t][:].indirect(offsets[:]))
+        xE_sb = [keep.tile([P, TABLE], F32, name=f"xE{t}", tag=f"table{t}") for t in range(LANES)]
+        for t in range(LANES):
+            nc.sync.dma_start(xE_sb[t][:], xE_rows[:, t, :])
+        x_grouped = keep.tile([P, SLOTS, LANES], BF16, name="x_grouped", align_bytes=64)
+        interleave(nc, "vector", x_grouped[:], x_listed[:])
+        x_codes = keep.tile([P, SLOTS], U32, name="x_codes", align_bytes=64)
+        x_scales = keep.tile([P, SLOTS], U8, name="x_scales", align_bytes=64)
+        nc.vector.quantize_mx(out=x_codes[:].bitcast(FP8X4), scales=x_scales[:], in_=x_grouped[:].rearrange("p c t -> p (c t)"))
+
+        pc_grouped = keep.tile([P, LANES, P, LANES], BF16, name="pc_grouped", tag="pc_grouped", align_bytes=64)
+        dealt = pc_grouped[:].rearrange("p t m j -> p m j t")
+        source = pc_sb[:].rearrange("p j (m t) -> p m j t", t=LANES)
+        nc.scalar.copy(out=dealt[:, : P // 2], in_=source[:, : P // 2])
+        nc.vector.tensor_copy(out=dealt[:, P // 2 :], in_=source[:, P // 2 :])
+        pc_codes = keep.tile([P, SLOTS], U32, name="pc_codes", align_bytes=64)
+        pc_scales = keep.tile([P, SLOTS], U8, name="pc_scales", align_bytes=64)
+        nc.vector.quantize_mx(out=pc_codes[:].bitcast(FP8X4), scales=pc_scales[:], in_=pc_grouped[:].rearrange("p t m j -> p (t m j)"))
+
+        er_listed = keep.tile([P, SLOTS], F32, name="er_listed", tag="pc_grouped", align_bytes=64)
+        nc.vector.tensor_copy(out=er_listed[:], in_=er_sb[:].indirect(offsets[:]))
+
+        k_sb = [keep.tile([P, SLOTS], F32, name=f"k{t}") for t in range(LANES)]
+        for t in range(LANES):
+            k_bank = psum.tile([P, SLOTS], F32, name=f"k_bank{t}", tag=f"k{t % 2}")
+            cols = slice(t * P, (t + 1) * P)
+            nc.tensor.matmul_mx(
+                out=k_bank[:],
+                lhsT=pc_codes[:, cols].bitcast(FP8X4),
+                lhsT_scale=pc_scales[:, cols],
+                rhs=x_codes[:].bitcast(FP8X4),
+                rhs_scale=x_scales[:],
+                start=True,
+                stop=True,
+            )
+            nc.scalar.copy(out=k_sb[t][:], in_=k_bank[:])
+
+        er_turned = psum.tile([P, BLOCKS, P], F32, name="er_turned", tag="spread0")
+        for b in range(BLOCKS):
+            nc.tensor.transpose(er_turned[:, b, :], er_listed[:, b * P : (b + 1) * P], identity[:])
+        er_columns = keep.tile([P, BLOCKS], F32, name="er_columns")
+        nc.scalar.copy(out=er_columns[:], in_=er_turned[:, :, 0])
+
+        sums = [psum.tile([P, P], F32, name=f"sums{b}", tag=f"sums{b}") for b in range(BLOCKS)]
+        for b in range(BLOCKS):
+            nc.tensor.matmul(sums[b][:], identity[:], identity[:], start=True, stop=False, is_transpose=True)
+        for t in range(LANES):
+            last = t == LANES - 1
+            q = keep.tile([P, SLOTS], F32, name=f"q{t}")
+            if last:
+                for h in range(2):
+                    cols = slice(h * HALF, (h + 1) * HALF)
+                    nc.vector.tensor_tensor(q[:, cols], xE_sb[t][:].indirect(half_offsets[h]), k_sb[t][:, cols], MULT)
+            else:
+                nc.vector.tensor_tensor(q[:], xE_sb[t][:].indirect(offsets[:]), k_sb[t][:], MULT)
+            for b in range(BLOCKS):
+                nc.tensor.matmul(sums[b][:], q[:, b * P : (b + 1) * P], identity[:], start=False, stop=last, is_transpose=True)
+
+        factor = keep.tile([P, SLOTS], F32, name="factor")
+        summed = keep.tile([P, BLOCKS, P], F32, name="summed")
+        for h in range(2):
+            denominator = keep.tile([P, 2], F32, name=f"denominator{h}")
+            for i in range(2):
+                nc.scalar.activation(out=summed[:, 2 * h + i, :], in_=sums[2 * h + i][:], func=COPY, accum_out=denominator[:, i : i + 1])
+            inverse = keep.tile([P, 2], F32, name=f"inverse{h}")
+            nc.vector.reciprocal(out=inverse[:], in_=denominator[:])
+            factor_columns = keep.tile([P, 2], F32, name=f"factor_columns{h}")
+            nc.vector.tensor_tensor(factor_columns[:], inverse[:], er_columns[:, 2 * h : 2 * h + 2], MULT)
+            spread = psum.tile([P, 2, P], F32, name=f"spread{h}", tag=f"spread{h}")
+            for i in range(2):
+                nc.tensor.transpose(spread[:, i, :], factor_columns[:, i : i + 1].to_broadcast([P, P]), identity[:])
+            nc.scalar.copy(out=factor[:, h * HALF : (h + 1) * HALF], in_=spread[:].rearrange("p i m -> p (i m)"))
+
+        rounded = [keep.tile([P, LANES, width], BF16, name=f"rounded{n}") for n, (first, width, e1, e2) in enumerate(CHUNKS)]
+        for t in range(LANES):
+            if t == 0:
+                for h in range(2):
+                    cols = slice(h * HALF, (h + 1) * HALF)
+                    nc.vector.tensor_tensor(windows[t][:].indirect(half_offsets[h]), k_sb[t][:, cols], factor[:, cols], MULT)
+            else:
+                nc.vector.tensor_tensor(windows[t][:].indirect(offsets[:]), k_sb[t][:], factor[:], MULT)
+            nc.sync.dma_start(out_rows[:, t, :], windows[t][:])
+            for n, (first, width, rounds_last, weaves) in enumerate(CHUNKS):
+                engine = rounds_last if t == LANES - 1 else "scalar"
+                copy_on(nc, engine, rounded[n][:, t, :], windows[t][:, first : first + width])
+
+        words_out = out_1[0].rearrange("p c l -> p (c l)").bitcast(I32)
+        out_scales = keep.tile([P, TABLE], U8, name="out_scales", align_bytes=64)
+        grouped = [keep.tile([P, width, LANES], BF16, name=f"grouped{n}", align_bytes=64) for n, (first, width, e1, e2) in enumerate(CHUNKS)]
+        for n, (first, width, rounds_last, weaves) in enumerate(CHUNKS):
+            interleave(nc, weaves, grouped[n][:], rounded[n][:])
+        for n in (1, 0, 2, 3, 4):
+            first, width = CHUNKS[n][:2]
+            codes = keep.tile([P, width], U32, name=f"codes{n}", align_bytes=64)
+            nc.vector.quantize_mx(
+                out=codes[:].bitcast(FP8X4),
+                scales=out_scales[:, first : first + width],
+                in_=grouped[n][:].rearrange("p c t -> p (c t)"),
+            )
+            nc.sync.dma_start(words_out[:, first : first + width], codes[:].bitcast(I32))
+        scales_out = out_2[0].bitcast(I32)
+        for quadrant in range(4):
+            queue = nc.sync if quadrant % 2 == 0 else nc.scalar
+            queue.dma_start(scales_out[4 * quadrant : 4 * quadrant + 4, :], out_scales[32 * quadrant : 32 * quadrant + 4, :].bitcast(I32))

@@ -21,13 +21,8 @@ HALF = SLOTS // 2
 BLOCKS = SLOTS // P
 FLOPS = 2 * 512 * 512 * 512
 
-CHUNKS = (
-    (0, 512, "scalar", "scalar"),
-    (512, 512, "vector", "vector"),
-    (1024, 512, "vector", "vector"),
-    (1536, 256, "vector", "scalar"),
-    (1792, 256, "vector", "scalar"),
-)
+CHUNK = 256
+CHUNKS = TABLE // CHUNK
 
 
 def copy_on(nc, engine, out, in_):
@@ -116,6 +111,11 @@ def tile_attend_grls_pl_kernel(tc, Pc, xT, xE, er, offs, out_0, out_1, out_2):
             nc.tensor.transpose(er_turned[:, b, :], er_listed[:, b * P : (b + 1) * P], identity[:])
         er_columns = keep.tile([P, BLOCKS], F32, name="er_columns")
         nc.scalar.copy(out=er_columns[:], in_=er_turned[:, :, 0])
+        er_spread = psum.tile([P, 2, P], F32, name="er_spread", tag="spread1")
+        for i in range(2):
+            nc.tensor.transpose(er_spread[:, i, :], er_columns[:, i : i + 1].to_broadcast([P, P]), identity[:])
+        er_rows = keep.tile([P, HALF], F32, name="er_rows")
+        nc.scalar.copy(out=er_rows[:], in_=er_spread[:].rearrange("p i m -> p (i m)"))
 
         sums = [psum.tile([P, P], F32, name=f"sums{b}", tag=f"sums{b}") for b in range(BLOCKS)]
         for b in range(BLOCKS):
@@ -124,9 +124,9 @@ def tile_attend_grls_pl_kernel(tc, Pc, xT, xE, er, offs, out_0, out_1, out_2):
             last = t == LANES - 1
             q = keep.tile([P, SLOTS], F32, name=f"q{t}")
             if last:
-                for h in range(2):
-                    cols = slice(h * HALF, (h + 1) * HALF)
-                    nc.vector.tensor_tensor(q[:, cols], xE_sb[t][:].indirect(half_offsets[h]), k_sb[t][:, cols], MULT)
+                for first, end in ((b * P, (b + 1) * P) for b in range(BLOCKS)):
+                    piece = offsets[:, first // 16 : end // 16]
+                    nc.vector.tensor_tensor(q[:, first:end], xE_sb[t][:].indirect(piece), k_sb[t][:, first:end], MULT)
             else:
                 nc.vector.tensor_tensor(q[:], xE_sb[t][:].indirect(offsets[:]), k_sb[t][:], MULT)
             for b in range(BLOCKS):
@@ -138,16 +138,29 @@ def tile_attend_grls_pl_kernel(tc, Pc, xT, xE, er, offs, out_0, out_1, out_2):
             denominator = keep.tile([P, 2], F32, name=f"denominator{h}")
             for i in range(2):
                 nc.scalar.activation(out=summed[:, 2 * h + i, :], in_=sums[2 * h + i][:], func=COPY, accum_out=denominator[:, i : i + 1])
-            inverse = keep.tile([P, 2], F32, name=f"inverse{h}")
-            nc.vector.reciprocal(out=inverse[:], in_=denominator[:])
-            factor_columns = keep.tile([P, 2], F32, name=f"factor_columns{h}")
-            nc.vector.tensor_tensor(factor_columns[:], inverse[:], er_columns[:, 2 * h : 2 * h + 2], MULT)
             spread = psum.tile([P, 2, P], F32, name=f"spread{h}", tag=f"spread{h}")
-            for i in range(2):
-                nc.tensor.transpose(spread[:, i, :], factor_columns[:, i : i + 1].to_broadcast([P, P]), identity[:])
-            nc.scalar.copy(out=factor[:, h * HALF : (h + 1) * HALF], in_=spread[:].rearrange("p i m -> p (i m)"))
+            cols = slice(h * HALF, (h + 1) * HALF)
+            if h == 0:
+                inverse = keep.tile([P, 2], F32, name="inverse0")
+                nc.vector.reciprocal(out=inverse[:], in_=denominator[:])
+                for i in range(2):
+                    nc.tensor.transpose(spread[:, i, :], inverse[:, i : i + 1].to_broadcast([P, P]), identity[:])
+                nc.vector.tensor_tensor(factor[:, cols], spread[:].rearrange("p i m -> p (i m)"), er_rows[:], MULT)
+            else:
+                inverse = keep.tile([P, 2], F32, name="inverse1")
+                nc.vector.reciprocal(out=inverse[:], in_=denominator[:])
+                factor_columns = keep.tile([P, 2], F32, name="factor_columns")
+                for i in range(2):
+                    nc.scalar.activation(out=factor_columns[:, i : i + 1], in_=inverse[:, i : i + 1], func=COPY, scale=er_columns[:, 2 + i : 3 + i])
+                    nc.tensor.transpose(spread[:, i, :], factor_columns[:, i : i + 1].to_broadcast([P, P]), identity[:])
+                nc.scalar.copy(out=factor[:, cols], in_=spread[:].rearrange("p i m -> p (i m)"))
 
-        rounded = [keep.tile([P, LANES, width], BF16, name=f"rounded{n}") for n, (first, width, e1, e2) in enumerate(CHUNKS)]
+        pairs = keep.tile([P, CHUNKS, 2, CHUNK, 2], BF16, name="pairs")
+
+        def write_lane(engine, t, first, last):
+            source = windows[t][:, first * CHUNK : last * CHUNK].rearrange("p (n c) -> p n c", c=CHUNK)
+            copy_on(nc, engine, pairs[:, first:last, t // 2, :, t % 2], source)
+
         for t in range(LANES):
             if t == 0:
                 for h in range(2):
@@ -156,24 +169,58 @@ def tile_attend_grls_pl_kernel(tc, Pc, xT, xE, er, offs, out_0, out_1, out_2):
             else:
                 nc.vector.tensor_tensor(windows[t][:].indirect(offsets[:]), k_sb[t][:], factor[:], MULT)
             nc.sync.dma_start(out_rows[:, t, :], windows[t][:])
-            for n, (first, width, rounds_last, weaves) in enumerate(CHUNKS):
-                engine = rounds_last if t == LANES - 1 else "scalar"
-                copy_on(nc, engine, rounded[n][:, t, :], windows[t][:, first : first + width])
+            if t < 2:
+                write_lane("scalar", t, 0, CHUNKS)
+            if t == 2:
+                write_lane("scalar", t, 1, CHUNKS)
 
         words_out = out_1[0].rearrange("p c l -> p (c l)").bitcast(I32)
         out_scales = keep.tile([P, TABLE], U8, name="out_scales", align_bytes=64)
-        grouped = [keep.tile([P, width, LANES], BF16, name=f"grouped{n}", align_bytes=64) for n, (first, width, e1, e2) in enumerate(CHUNKS)]
-        for n, (first, width, rounds_last, weaves) in enumerate(CHUNKS):
-            interleave(nc, weaves, grouped[n][:], rounded[n][:])
-        for n in (1, 0, 2, 3, 4):
-            first, width = CHUNKS[n][:2]
-            codes = keep.tile([P, width], U32, name=f"codes{n}", align_bytes=64)
+        grouped = keep.tile([P, TABLE * LANES], BF16, name="grouped", align_bytes=64)
+        codes = keep.tile([P, TABLE], U32, name="codes", align_bytes=64)
+
+        def merge(engine, first, last):
+            word = U32 if engine == "scalar" else I32
+            source = pairs[:, first:last].rearrange("p n u c v -> p n u (c v)").bitcast(word).rearrange("p n u c -> p n c u")
+            target = grouped[:, first * CHUNK * LANES : last * CHUNK * LANES]
+            copy_on(nc, engine, target.bitcast(word).rearrange("p (n c u) -> p n c u", c=CHUNK, u=2), source)
+
+        def quantise(first, last):
+            cols = slice(first * CHUNK, last * CHUNK)
             nc.vector.quantize_mx(
-                out=codes[:].bitcast(FP8X4),
-                scales=out_scales[:, first : first + width],
-                in_=grouped[n][:].rearrange("p c t -> p (c t)"),
+                out=codes[:, cols].bitcast(FP8X4),
+                scales=out_scales[:, cols],
+                in_=grouped[:, first * CHUNK * LANES : last * CHUNK * LANES],
             )
-            nc.sync.dma_start(words_out[:, first : first + width], codes[:].bitcast(I32))
+
+        def store(first, last):
+            cols = slice(first * CHUNK, last * CHUNK)
+            nc.sync.dma_start(words_out[:, cols], codes[:, cols].bitcast(I32))
+
+        write_lane("vector", 2, 0, 1)
+        write_lane("vector", 3, 0, 1)
+        write_lane("scalar", 3, 1, 3)
+        write_lane("scalar", 3, 3, 5)
+        merge("vector", 0, 1)
+        merge("vector", 1, 2)
+        merge("vector", 2, 3)
+        merge("scalar", 3, 4)
+        quantise(0, 1)
+        merge("vector", 4, 5)
+        write_lane("scalar", 3, 5, 7)
+        quantise(1, 3)
+        store(0, 3)
+        write_lane("scalar", 3, 7, 8)
+        quantise(3, 5)
+        store(3, 5)
+        merge("scalar", 6, 7)
+        merge("vector", 5, 6)
+        merge("vector", 7, 8)
+        quantise(5, 6)
+        quantise(6, 7)
+        store(5, 7)
+        quantise(7, 8)
+        store(7, 8)
         scales_out = out_2[0].bitcast(I32)
         for quadrant in range(4):
             queue = nc.sync if quadrant % 2 == 0 else nc.scalar

@@ -32,10 +32,6 @@ def copy_on(nc, engine, out, in_):
         nc.vector.tensor_copy(out=out, in_=in_)
 
 
-def interleave(nc, engine, grouped, rows):
-    copy_on(nc, engine, grouped.rearrange("p (c i) t -> p c t i", i=4), rows.rearrange("p t (c i) -> p c t i", i=4))
-
-
 def tile_attend_grls_pl_kernel(tc, Pc, xT, xE, er, offs, out_0, out_1, out_2):
     nc = tc.nc
     with ExitStack() as ctx:
@@ -55,29 +51,46 @@ def tile_attend_grls_pl_kernel(tc, Pc, xT, xE, er, offs, out_0, out_1, out_2):
         er_sb = keep.tile([P, TABLE], F32, name="er_sb")
         windows = [keep.tile([P, TABLE], F32, name=f"window{t}") for t in range(LANES)]
 
+        er_upright = keep.tile([P, TABLE // P], F32, name="er_upright")
+        nc.sync.dma_start(er_upright[:], er[0].rearrange("(p j) -> p j", p=P))
         for t in range(LANES):
             nc.sync.dma_start(xT_sb[t][:], xT_rows[:, t, :])
         nc.sync.dma_start(pc_sb[:], Pc.rearrange("(p j) e -> p j e", j=LANES))
 
-        nc.vector.memset(er_sb[:], 0.0)
-        nc.sync.dma_start(er_sb[0:1, :], er[0:1, :])
         nc.vector.memset(windows[0][:], 0.0)
         identity = keep.tile([P, P], F32, name="identity")
         make_identity(nc, identity[:])
         for t in range(1, LANES):
             nc.gpsimd.memset(windows[t][:], 0.0)
 
-        x_listed = keep.tile([P, LANES, SLOTS], BF16, name="x_listed")
-        for t in range(LANES):
+        er_places = er_sb[:].rearrange("p (m j) -> p m j", m=P)
+        for n, tag in enumerate(("k0", "k1", "spread0", "spread1")):
+            er_wide = psum.tile([P, BLOCKS, P], F32, name=f"er_wide{n}", tag=tag)
+            for b in range(BLOCKS):
+                column = BLOCKS * n + b
+                nc.tensor.transpose(er_wide[:, b, :], er_upright[:, column : column + 1].to_broadcast([P, P]), identity[:])
+            nc.scalar.activation(out=er_places[:, :, BLOCKS * n : BLOCKS * (n + 1)], in_=er_wide[:].rearrange("p b m -> p m b"), func=COPY)
+
+        halves = [slice(h * HALF, (h + 1) * HALF) for h in range(2)]
+        x_listed = keep.tile([P, LANES - 1, SLOTS], BF16, name="x_listed")
+        x_last = keep.tile([P, SLOTS], BF16, name="x_last")
+        x_grouped = keep.tile([P, SLOTS, LANES], BF16, name="x_grouped", align_bytes=64)
+        for t in range(LANES - 1):
             nc.vector.tensor_copy(out=x_listed[:, t, :], in_=xT_sb[t][:].indirect(offsets[:]))
+        nc.vector.tensor_copy(
+            out=x_grouped[:, :, : LANES - 1].rearrange("p (c i) t -> p c t i", i=4), in_=x_listed[:].rearrange("p t (c i) -> p c t i", i=4)
+        )
+        for h in range(2):
+            nc.vector.tensor_copy(out=x_last[:, halves[h]], in_=xT_sb[LANES - 1][:].indirect(half_offsets[h]))
+        for cols in halves:
+            nc.vector.tensor_copy(out=x_grouped[:, cols, LANES - 1], in_=x_last[:, cols])
         xE_sb = [keep.tile([P, TABLE], F32, name=f"xE{t}", tag=f"table{t}") for t in range(LANES)]
         for t in range(LANES):
             nc.sync.dma_start(xE_sb[t][:], xE_rows[:, t, :])
-        x_grouped = keep.tile([P, SLOTS, LANES], BF16, name="x_grouped", align_bytes=64)
-        interleave(nc, "vector", x_grouped[:], x_listed[:])
         x_codes = keep.tile([P, SLOTS], U32, name="x_codes", align_bytes=64)
         x_scales = keep.tile([P, SLOTS], U8, name="x_scales", align_bytes=64)
-        nc.vector.quantize_mx(out=x_codes[:].bitcast(FP8X4), scales=x_scales[:], in_=x_grouped[:].rearrange("p c t -> p (c t)"))
+        for cols in halves:
+            nc.vector.quantize_mx(out=x_codes[:, cols].bitcast(FP8X4), scales=x_scales[:, cols], in_=x_grouped[:, cols, :].rearrange("p c t -> p (c t)"))
 
         pc_grouped = keep.tile([P, LANES, P, LANES], BF16, name="pc_grouped", tag="pc_grouped", align_bytes=64)
         dealt = pc_grouped[:].rearrange("p t m j -> p m j t")
@@ -86,7 +99,11 @@ def tile_attend_grls_pl_kernel(tc, Pc, xT, xE, er, offs, out_0, out_1, out_2):
         nc.vector.tensor_copy(out=dealt[:, P // 2 :], in_=source[:, P // 2 :])
         pc_codes = keep.tile([P, SLOTS], U32, name="pc_codes", align_bytes=64)
         pc_scales = keep.tile([P, SLOTS], U8, name="pc_scales", align_bytes=64)
-        nc.vector.quantize_mx(out=pc_codes[:].bitcast(FP8X4), scales=pc_scales[:], in_=pc_grouped[:].rearrange("p t m j -> p (t m j)"))
+        for first, end in ((0, 1), (1, 2), (2, LANES)):
+            cols = slice(first * P, end * P)
+            nc.vector.quantize_mx(
+                out=pc_codes[:, cols].bitcast(FP8X4), scales=pc_scales[:, cols], in_=pc_grouped[:, first:end].rearrange("p t m j -> p (t m j)")
+            )
 
         er_listed = keep.tile([P, SLOTS], F32, name="er_listed", tag="pc_grouped", align_bytes=64)
         nc.vector.tensor_copy(out=er_listed[:], in_=er_sb[:].indirect(offsets[:]))
@@ -106,16 +123,11 @@ def tile_attend_grls_pl_kernel(tc, Pc, xT, xE, er, offs, out_0, out_1, out_2):
             )
             nc.scalar.copy(out=k_sb[t][:], in_=k_bank[:])
 
-        er_turned = psum.tile([P, BLOCKS, P], F32, name="er_turned", tag="spread0")
-        for b in range(BLOCKS):
-            nc.tensor.transpose(er_turned[:, b, :], er_listed[:, b * P : (b + 1) * P], identity[:])
-        er_columns = keep.tile([P, BLOCKS], F32, name="er_columns")
-        nc.scalar.copy(out=er_columns[:], in_=er_turned[:, :, 0])
-        er_spread = psum.tile([P, 2, P], F32, name="er_spread", tag="spread1")
+        er_turned = psum.tile([P, 2, P], F32, name="er_turned", tag="spread0")
         for i in range(2):
-            nc.tensor.transpose(er_spread[:, i, :], er_columns[:, i : i + 1].to_broadcast([P, P]), identity[:])
-        er_rows = keep.tile([P, HALF], F32, name="er_rows")
-        nc.scalar.copy(out=er_rows[:], in_=er_spread[:].rearrange("p i m -> p (i m)"))
+            nc.tensor.transpose(er_turned[:, i, :], er_listed[:, HALF + i * P : HALF + (i + 1) * P], identity[:])
+        er_columns = keep.tile([P, 2], F32, name="er_columns")
+        nc.scalar.copy(out=er_columns[:], in_=er_turned[:, :, 0])
 
         sums = [psum.tile([P, P], F32, name=f"sums{b}", tag=f"sums{b}") for b in range(BLOCKS)]
         for b in range(BLOCKS):
@@ -145,13 +157,13 @@ def tile_attend_grls_pl_kernel(tc, Pc, xT, xE, er, offs, out_0, out_1, out_2):
                 nc.vector.reciprocal(out=inverse[:], in_=denominator[:])
                 for i in range(2):
                     nc.tensor.transpose(spread[:, i, :], inverse[:, i : i + 1].to_broadcast([P, P]), identity[:])
-                nc.vector.tensor_tensor(factor[:, cols], spread[:].rearrange("p i m -> p (i m)"), er_rows[:], MULT)
+                nc.vector.tensor_tensor(factor[:, cols], spread[:].rearrange("p i m -> p (i m)"), er_listed[:, cols], MULT)
             else:
                 inverse = keep.tile([P, 2], F32, name="inverse1")
                 nc.vector.reciprocal(out=inverse[:], in_=denominator[:])
                 factor_columns = keep.tile([P, 2], F32, name="factor_columns")
                 for i in range(2):
-                    nc.scalar.activation(out=factor_columns[:, i : i + 1], in_=inverse[:, i : i + 1], func=COPY, scale=er_columns[:, 2 + i : 3 + i])
+                    nc.scalar.activation(out=factor_columns[:, i : i + 1], in_=inverse[:, i : i + 1], func=COPY, scale=er_columns[:, i : i + 1])
                     nc.tensor.transpose(spread[:, i, :], factor_columns[:, i : i + 1].to_broadcast([P, P]), identity[:])
                 nc.scalar.copy(out=factor[:, cols], in_=spread[:].rearrange("p i m -> p (i m)"))
 
@@ -175,7 +187,7 @@ def tile_attend_grls_pl_kernel(tc, Pc, xT, xE, er, offs, out_0, out_1, out_2):
                 write_lane("scalar", t, 1, CHUNKS)
 
         words_out = out_1[0].rearrange("p c l -> p (c l)").bitcast(I32)
-        out_scales = keep.tile([P, TABLE], U8, name="out_scales", align_bytes=64)
+        out_scales = keep.tile([P, 2 * CHUNK], U8, name="out_scales", align_bytes=64)
         grouped = keep.tile([P, TABLE * LANES], BF16, name="grouped", align_bytes=64)
         codes = keep.tile([P, TABLE], U32, name="codes", align_bytes=64)
 
@@ -189,7 +201,7 @@ def tile_attend_grls_pl_kernel(tc, Pc, xT, xE, er, offs, out_0, out_1, out_2):
             cols = slice(first * CHUNK, last * CHUNK)
             nc.vector.quantize_mx(
                 out=codes[:, cols].bitcast(FP8X4),
-                scales=out_scales[:, cols],
+                scales=out_scales[4 * (first // 2) :, first % 2 * CHUNK : (first % 2 + last - first) * CHUNK],
                 in_=grouped[:, first * CHUNK * LANES : last * CHUNK * LANES],
             )
 
@@ -199,29 +211,30 @@ def tile_attend_grls_pl_kernel(tc, Pc, xT, xE, er, offs, out_0, out_1, out_2):
 
         write_lane("vector", 2, 0, 1)
         write_lane("vector", 3, 0, 1)
-        write_lane("scalar", 3, 1, 3)
-        write_lane("scalar", 3, 3, 5)
+        write_lane("scalar", 3, 2, 4)
+        write_lane("scalar", 3, 4, 6)
         merge("vector", 0, 1)
-        merge("vector", 1, 2)
         merge("vector", 2, 3)
-        merge("scalar", 3, 4)
+        merge("vector", 3, 4)
+        merge("scalar", 4, 5)
         quantise(0, 1)
-        merge("vector", 4, 5)
-        write_lane("scalar", 3, 5, 7)
-        quantise(1, 3)
-        store(0, 3)
-        write_lane("scalar", 3, 7, 8)
-        quantise(3, 5)
-        store(3, 5)
-        merge("scalar", 6, 7)
+        store(0, 1)
         merge("vector", 5, 6)
+        write_lane("scalar", 3, 6, 8)
+        quantise(2, 4)
+        store(2, 4)
+        write_lane("scalar", 3, 1, 2)
+        quantise(4, 6)
+        store(4, 6)
+        merge("scalar", 6, 7)
         merge("vector", 7, 8)
-        quantise(5, 6)
-        quantise(6, 7)
-        store(5, 7)
+        merge("vector", 1, 2)
         quantise(7, 8)
-        store(7, 8)
-        scales_out = out_2[0].bitcast(I32)
+        quantise(6, 7)
+        store(6, 8)
+        quantise(1, 2)
+        store(1, 2)
+        scales_out = out_2[0].bitcast(I32).rearrange("r (j c) -> j r c", j=4)
         for quadrant in range(4):
             queue = nc.sync if quadrant % 2 == 0 else nc.scalar
-            queue.dma_start(scales_out[4 * quadrant : 4 * quadrant + 4, :], out_scales[32 * quadrant : 32 * quadrant + 4, :].bitcast(I32))
+            queue.dma_start(scales_out[:, 4 * quadrant : 4 * quadrant + 4, :], out_scales[32 * quadrant : 32 * quadrant + 16, :].bitcast(I32))

@@ -21,8 +21,9 @@ HALF = SLOTS // 2
 BLOCKS = SLOTS // P
 FLOPS = 2 * 512 * 512 * 512
 
-CHUNK = 256
-CHUNKS = TABLE // CHUNK
+UNIT = 128
+UNITS = TABLE // UNIT
+PLANE = TABLE // 4
 
 
 def copy_on(nc, engine, out, in_):
@@ -146,32 +147,33 @@ def tile_attend_grls_pl_kernel(tc, Pc, xT, xE, er, offs, out_0, out_1, out_2):
 
         factor = keep.tile([P, SLOTS], F32, name="factor")
         summed = keep.tile([P, BLOCKS, P], F32, name="summed")
-        for h in range(2):
-            denominator = keep.tile([P, 2], F32, name=f"denominator{h}")
-            for i in range(2):
-                nc.scalar.activation(out=summed[:, 2 * h + i, :], in_=sums[2 * h + i][:], func=COPY, accum_out=denominator[:, i : i + 1])
-            spread = psum.tile([P, 2, P], F32, name=f"spread{h}", tag=f"spread{h}")
-            cols = slice(h * HALF, (h + 1) * HALF)
-            if h == 0:
-                inverse = keep.tile([P, 2], F32, name="inverse0")
-                nc.vector.reciprocal(out=inverse[:], in_=denominator[:])
-                for i in range(2):
-                    nc.tensor.transpose(spread[:, i, :], inverse[:, i : i + 1].to_broadcast([P, P]), identity[:])
-                nc.vector.tensor_tensor(factor[:, cols], spread[:].rearrange("p i m -> p (i m)"), er_listed[:, cols], MULT)
-            else:
-                inverse = keep.tile([P, 2], F32, name="inverse1")
-                nc.vector.reciprocal(out=inverse[:], in_=denominator[:])
-                factor_columns = keep.tile([P, 2], F32, name="factor_columns")
-                for i in range(2):
-                    nc.scalar.activation(out=factor_columns[:, i : i + 1], in_=inverse[:, i : i + 1], func=COPY, scale=er_columns[:, i : i + 1])
-                    nc.tensor.transpose(spread[:, i, :], factor_columns[:, i : i + 1].to_broadcast([P, P]), identity[:])
-                nc.scalar.copy(out=factor[:, cols], in_=spread[:].rearrange("p i m -> p (i m)"))
+        for b in range(2):
+            cols = slice(b * P, (b + 1) * P)
+            denominator = keep.tile([P, 1], F32, name=f"denominator{b}")
+            nc.scalar.activation(out=summed[:, b, :], in_=sums[b][:], func=COPY, accum_out=denominator[:])
+            inverse = keep.tile([P, 1], F32, name=f"inverse{b}")
+            nc.vector.reciprocal(out=inverse[:], in_=denominator[:])
+            spread = psum.tile([P, P], F32, name=f"spread{b}", tag=f"k{b}")
+            nc.tensor.transpose(spread[:], inverse[:].to_broadcast([P, P]), identity[:])
+            nc.vector.tensor_tensor(factor[:, cols], spread[:], er_listed[:, cols], MULT)
+        late_denominator = keep.tile([P, 2], F32, name="late_denominator")
+        for i in range(2):
+            nc.scalar.activation(out=summed[:, 2 + i, :], in_=sums[2 + i][:], func=COPY, accum_out=late_denominator[:, i : i + 1])
+        late_spread = psum.tile([P, 2, P], F32, name="late_spread", tag="spread1")
+        late_inverse = keep.tile([P, 2], F32, name="late_inverse")
+        nc.vector.reciprocal(out=late_inverse[:], in_=late_denominator[:])
+        factor_columns = keep.tile([P, 2], F32, name="factor_columns")
+        for i in range(2):
+            nc.scalar.activation(out=factor_columns[:, i : i + 1], in_=late_inverse[:, i : i + 1], func=COPY, scale=er_columns[:, i : i + 1])
+            nc.tensor.transpose(late_spread[:, i, :], factor_columns[:, i : i + 1].to_broadcast([P, P]), identity[:])
+        nc.scalar.copy(out=factor[:, HALF:], in_=late_spread[:].rearrange("p i m -> p (i m)"))
 
-        pairs = keep.tile([P, CHUNKS, 2, CHUNK, 2], BF16, name="pairs")
+        pairs = keep.tile([P, UNITS, 2, UNIT, 2], BF16, name="pairs")
 
         def write_lane(engine, t, first, last):
-            source = windows[t][:, first * CHUNK : last * CHUNK].rearrange("p (n c) -> p n c", c=CHUNK)
-            copy_on(nc, engine, pairs[:, first:last, t // 2, :, t % 2], source)
+            source = windows[t][:, first * UNIT : last * UNIT].rearrange("p (n h c) -> p h n c", h=2, c=UNIT // 2)
+            target = pairs[:, first:last, t // 2, :, t % 2].rearrange("p n (h c) -> p h n c", h=2)
+            copy_on(nc, engine, target, source)
 
         for t in range(LANES):
             if t == 0:
@@ -182,58 +184,60 @@ def tile_attend_grls_pl_kernel(tc, Pc, xT, xE, er, offs, out_0, out_1, out_2):
                 nc.vector.tensor_tensor(windows[t][:].indirect(offsets[:]), k_sb[t][:], factor[:], MULT)
             nc.sync.dma_start(out_rows[:, t, :], windows[t][:])
             if t < 2:
-                write_lane("scalar", t, 0, CHUNKS)
+                write_lane("scalar", t, 0, UNITS)
             if t == 2:
-                write_lane("scalar", t, 1, CHUNKS)
+                write_lane("scalar", t, 0, 1)
+                write_lane("scalar", t, 4, UNITS)
 
         words_out = out_1[0].rearrange("p c l -> p (c l)").bitcast(I32)
-        out_scales = keep.tile([P, 2 * CHUNK], U8, name="out_scales", align_bytes=64)
+        out_scales = keep.tile([P, PLANE], U8, name="out_scales", align_bytes=64)
         grouped = keep.tile([P, TABLE * LANES], BF16, name="grouped", align_bytes=64)
         codes = keep.tile([P, TABLE], U32, name="codes", align_bytes=64)
 
         def merge(engine, first, last):
             word = U32 if engine == "scalar" else I32
-            source = pairs[:, first:last].rearrange("p n u c v -> p n u (c v)").bitcast(word).rearrange("p n u c -> p n c u")
-            target = grouped[:, first * CHUNK * LANES : last * CHUNK * LANES]
-            copy_on(nc, engine, target.bitcast(word).rearrange("p (n c u) -> p n c u", c=CHUNK, u=2), source)
+            source = pairs[:, first:last].rearrange("p n u c v -> p n u (c v)").bitcast(word).rearrange("p n u (h c) -> p h n c u", h=2)
+            target = grouped[:, first * UNIT * LANES : last * UNIT * LANES]
+            copy_on(nc, engine, target.bitcast(word).rearrange("p (n h c u) -> p h n c u", h=2, c=UNIT // 2, u=2), source)
 
         def quantise(first, last):
-            cols = slice(first * CHUNK, last * CHUNK)
+            cols = slice(first * UNIT, last * UNIT)
+            plane, start = divmod(first * UNIT, PLANE)
             nc.vector.quantize_mx(
                 out=codes[:, cols].bitcast(FP8X4),
-                scales=out_scales[4 * (first // 2) :, first % 2 * CHUNK : (first % 2 + last - first) * CHUNK],
-                in_=grouped[:, first * CHUNK * LANES : last * CHUNK * LANES],
+                scales=out_scales[4 * plane :, start : start + (last - first) * UNIT],
+                in_=grouped[:, first * UNIT * LANES : last * UNIT * LANES],
             )
 
         def store(first, last):
-            cols = slice(first * CHUNK, last * CHUNK)
+            cols = slice(first * UNIT, last * UNIT)
             nc.sync.dma_start(words_out[:, cols], codes[:, cols].bitcast(I32))
 
-        write_lane("vector", 2, 0, 1)
-        write_lane("vector", 3, 0, 1)
-        write_lane("scalar", 3, 2, 4)
-        write_lane("scalar", 3, 4, 6)
-        merge("vector", 0, 1)
-        merge("vector", 2, 3)
-        merge("vector", 3, 4)
-        merge("scalar", 4, 5)
-        quantise(0, 1)
-        store(0, 1)
-        merge("vector", 5, 6)
-        write_lane("scalar", 3, 6, 8)
+        write_lane("vector", 2, 1, 4)
+        write_lane("vector", 3, 1, 2)
+        write_lane("vector", 3, 2, 4)
+        for first, last in ((0, 1), (4, 5), (5, 8), (8, 12), (12, 16)):
+            write_lane("scalar", 3, first, last)
+        for first, last in ((10, 12), (12, 14), (14, 15)):
+            merge("scalar", first, last)
+        merge("vector", 0, 2)
+        merge("vector", 2, 5)
+        quantise(0, 2)
+        merge("vector", 5, 8)
         quantise(2, 4)
-        store(2, 4)
-        write_lane("scalar", 3, 1, 2)
+        store(0, 4)
+        merge("vector", 8, 10)
         quantise(4, 6)
-        store(4, 6)
-        merge("scalar", 6, 7)
-        merge("vector", 7, 8)
-        merge("vector", 1, 2)
-        quantise(7, 8)
-        quantise(6, 7)
-        store(6, 8)
-        quantise(1, 2)
-        store(1, 2)
+        quantise(6, 8)
+        store(4, 8)
+        merge("vector", 15, 16)
+        quantise(8, 10)
+        quantise(10, 12)
+        store(8, 12)
+        quantise(12, 14)
+        store(12, 14)
+        quantise(14, 16)
+        store(14, 16)
         scales_out = out_2[0].bitcast(I32).rearrange("r (j c) -> j r c", j=4)
         for quadrant in range(4):
             queue = nc.sync if quadrant % 2 == 0 else nc.scalar

@@ -21,6 +21,7 @@ HALF = SLOTS // 2
 BLOCKS = SLOTS // P
 FLOPS = 2 * 512 * 512 * 512
 
+SCALAR_DEAL = 44
 UNIT = 128
 UNITS = TABLE // UNIT
 PLANE = TABLE // 4
@@ -74,7 +75,6 @@ def tile_attend_grls_pl_kernel(tc, Pc, xT, xE, er, offs, out_0, out_1, out_2):
 
         halves = [slice(h * HALF, (h + 1) * HALF) for h in range(2)]
         x_listed = keep.tile([P, LANES - 1, SLOTS], BF16, name="x_listed")
-        x_last = keep.tile([P, SLOTS], BF16, name="x_last")
         x_grouped = keep.tile([P, SLOTS, LANES], BF16, name="x_grouped", align_bytes=64)
         for t in range(LANES - 1):
             nc.vector.tensor_copy(out=x_listed[:, t, :], in_=xT_sb[t][:].indirect(offsets[:]))
@@ -82,9 +82,7 @@ def tile_attend_grls_pl_kernel(tc, Pc, xT, xE, er, offs, out_0, out_1, out_2):
             out=x_grouped[:, :, : LANES - 1].rearrange("p (c i) t -> p c t i", i=4), in_=x_listed[:].rearrange("p t (c i) -> p c t i", i=4)
         )
         for h in range(2):
-            nc.vector.tensor_copy(out=x_last[:, halves[h]], in_=xT_sb[LANES - 1][:].indirect(half_offsets[h]))
-        for cols in halves:
-            nc.vector.tensor_copy(out=x_grouped[:, cols, LANES - 1], in_=x_last[:, cols])
+            nc.vector.tensor_copy(out=x_grouped[:, halves[h], LANES - 1], in_=xT_sb[LANES - 1][:].indirect(half_offsets[h]))
         xE_sb = [keep.tile([P, TABLE], F32, name=f"xE{t}", tag=f"table{t}") for t in range(LANES)]
         for t in range(LANES):
             nc.sync.dma_start(xE_sb[t][:], xE_rows[:, t, :])
@@ -96,8 +94,8 @@ def tile_attend_grls_pl_kernel(tc, Pc, xT, xE, er, offs, out_0, out_1, out_2):
         pc_grouped = keep.tile([P, LANES, P, LANES], BF16, name="pc_grouped", tag="pc_grouped", align_bytes=64)
         dealt = pc_grouped[:].rearrange("p t m j -> p m j t")
         source = pc_sb[:].rearrange("p j (m t) -> p m j t", t=LANES)
-        nc.scalar.copy(out=dealt[:, : P // 2], in_=source[:, : P // 2])
-        nc.vector.tensor_copy(out=dealt[:, P // 2 :], in_=source[:, P // 2 :])
+        nc.scalar.copy(out=dealt[:, :SCALAR_DEAL], in_=source[:, :SCALAR_DEAL])
+        nc.vector.tensor_copy(out=dealt[:, SCALAR_DEAL:], in_=source[:, SCALAR_DEAL:])
         pc_codes = keep.tile([P, SLOTS], U32, name="pc_codes", align_bytes=64)
         pc_scales = keep.tile([P, SLOTS], U8, name="pc_scales", align_bytes=64)
         for first, end in ((0, 1), (1, 2), (2, LANES)):
@@ -106,27 +104,28 @@ def tile_attend_grls_pl_kernel(tc, Pc, xT, xE, er, offs, out_0, out_1, out_2):
                 out=pc_codes[:, cols].bitcast(FP8X4), scales=pc_scales[:, cols], in_=pc_grouped[:, first:end].rearrange("p t m j -> p (t m j)")
             )
 
-        er_listed = keep.tile([P, SLOTS], F32, name="er_listed", tag="pc_grouped", align_bytes=64)
-        nc.vector.tensor_copy(out=er_listed[:], in_=er_sb[:].indirect(offsets[:]))
+        er_second = keep.tile([P, HALF], F32, name="er_second", tag="pc_grouped", align_bytes=64)
+        nc.vector.tensor_copy(out=er_second[:], in_=er_sb[:].indirect(half_offsets[1]))
 
         k_sb = [keep.tile([P, SLOTS], F32, name=f"k{t}") for t in range(LANES)]
-        for t in range(LANES):
-            k_bank = psum.tile([P, SLOTS], F32, name=f"k_bank{t}", tag=f"k{t % 2}")
+        pieces = [(0, halves[0], "k0"), (0, halves[1], "spread1")] + [(t, slice(0, SLOTS), f"k{t % 2}") for t in range(1, LANES)]
+        for n, (t, slots, tag) in enumerate(pieces):
+            k_bank = psum.tile([P, slots.stop - slots.start], F32, name=f"k_bank{n}", tag=tag)
             cols = slice(t * P, (t + 1) * P)
             nc.tensor.matmul_mx(
                 out=k_bank[:],
                 lhsT=pc_codes[:, cols].bitcast(FP8X4),
                 lhsT_scale=pc_scales[:, cols],
-                rhs=x_codes[:].bitcast(FP8X4),
-                rhs_scale=x_scales[:],
+                rhs=x_codes[:, slots].bitcast(FP8X4),
+                rhs_scale=x_scales[:, slots],
                 start=True,
                 stop=True,
             )
-            nc.scalar.copy(out=k_sb[t][:], in_=k_bank[:])
+            nc.scalar.copy(out=k_sb[t][:, slots], in_=k_bank[:])
 
         er_turned = psum.tile([P, 2, P], F32, name="er_turned", tag="spread0")
         for i in range(2):
-            nc.tensor.transpose(er_turned[:, i, :], er_listed[:, HALF + i * P : HALF + (i + 1) * P], identity[:])
+            nc.tensor.transpose(er_turned[:, i, :], er_second[:, i * P : (i + 1) * P], identity[:])
         er_columns = keep.tile([P, 2], F32, name="er_columns")
         nc.scalar.copy(out=er_columns[:], in_=er_turned[:, :, 0])
 
@@ -140,8 +139,14 @@ def tile_attend_grls_pl_kernel(tc, Pc, xT, xE, er, offs, out_0, out_1, out_2):
                 for first, end in ((b * P, (b + 1) * P) for b in range(BLOCKS)):
                     piece = offsets[:, first // 16 : end // 16]
                     nc.vector.tensor_tensor(q[:, first:end], xE_sb[t][:].indirect(piece), k_sb[t][:, first:end], MULT)
+            elif t == 0:
+                for h in range(2):
+                    nc.vector.tensor_tensor(q[:, halves[h]], xE_sb[t][:].indirect(half_offsets[h]), k_sb[t][:, halves[h]], MULT)
             else:
                 nc.vector.tensor_tensor(q[:], xE_sb[t][:].indirect(offsets[:]), k_sb[t][:], MULT)
+            if t == 1:
+                er_first = keep.tile([P, HALF], F32, name="er_first", tag="table1")
+                nc.vector.tensor_copy(out=er_first[:], in_=er_sb[:].indirect(half_offsets[0]))
             for b in range(BLOCKS):
                 nc.tensor.matmul(sums[b][:], q[:, b * P : (b + 1) * P], identity[:], start=False, stop=last, is_transpose=True)
 
@@ -155,7 +160,7 @@ def tile_attend_grls_pl_kernel(tc, Pc, xT, xE, er, offs, out_0, out_1, out_2):
             nc.vector.reciprocal(out=inverse[:], in_=denominator[:])
             spread = psum.tile([P, P], F32, name=f"spread{b}", tag=f"k{b}")
             nc.tensor.transpose(spread[:], inverse[:].to_broadcast([P, P]), identity[:])
-            nc.vector.tensor_tensor(factor[:, cols], spread[:], er_listed[:, cols], MULT)
+            nc.vector.tensor_tensor(factor[:, cols], spread[:], er_first[:, cols], MULT)
         late_denominator = keep.tile([P, 2], F32, name="late_denominator")
         for i in range(2):
             nc.scalar.activation(out=summed[:, 2 + i, :], in_=sums[2 + i][:], func=COPY, accum_out=late_denominator[:, i : i + 1])

@@ -18,10 +18,10 @@ LANES = 4
 SLOTS = 512
 TABLE = 2048
 HALF = SLOTS // 2
-BLOCKS = SLOTS // P
+RUNS = SLOTS // P
 FLOPS = 2 * 512 * 512 * 512
 
-SCALAR_DEAL = 44
+SCALAR_DEAL = 72
 UNIT = 128
 UNITS = TABLE // UNIT
 PLANE = TABLE // 4
@@ -42,60 +42,71 @@ def tile_attend_grls_pl_kernel(tc, Pc, xT, xE, er, offs, out_0, out_1, out_2):
 
         offsets = keep.tile([P, SLOTS // 16], U16, name="offsets")
         nc.sync.dma_start(offsets[:], offs)
-        half_offsets = [offsets[:, h * HALF // 16 : (h + 1) * HALF // 16] for h in range(2)]
+        halves = [slice(h * HALF, (h + 1) * HALF) for h in range(2)]
+        runs = [slice(b * P, (b + 1) * P) for b in range(RUNS)]
 
+        def listed(window, slots):
+            return window.indirect(offsets[:, slots.start // 16 : slots.stop // 16])
+
+        every = slice(0, SLOTS)
         xT_rows = xT.rearrange("(p t) c -> p t c", t=LANES)
         xE_rows = xE.rearrange("(p t) c -> p t c", t=LANES)
         out_rows = out_0.rearrange("(p t) c -> p t c", t=LANES)
 
-        xT_sb = [keep.tile([P, TABLE], F32, name=f"xT{t}", tag=f"table{t}") for t in range(LANES)]
-        pc_sb = keep.tile([P, LANES, SLOTS], F32, name="pc_sb")
-        er_sb = keep.tile([P, TABLE], F32, name="er_sb")
-        windows = [keep.tile([P, TABLE], F32, name=f"window{t}") for t in range(LANES)]
-
         er_upright = keep.tile([P, TABLE // P], F32, name="er_upright")
         nc.sync.dma_start(er_upright[:], er[0].rearrange("(p j) -> p j", p=P))
-        for t in range(LANES):
-            nc.sync.dma_start(xT_sb[t][:], xT_rows[:, t, :])
+        xT_sb = [keep.tile([P, 2, TABLE], F32, name=f"xT{u}") for u in range(2)]
+        for u in range(2):
+            nc.sync.dma_start(xT_sb[u][:], xT_rows[:, 2 * u : 2 * u + 2, :])
+        pc_sb = keep.tile([P, LANES, SLOTS], F32, name="pc_sb")
         nc.sync.dma_start(pc_sb[:], Pc.rearrange("(p j) e -> p j e", j=LANES))
-
-        nc.vector.memset(windows[0][:], 0.0)
-        identity = keep.tile([P, P], F32, name="identity")
-        make_identity(nc, identity[:])
-        for t in range(1, LANES):
-            nc.gpsimd.memset(windows[t][:], 0.0)
-
-        er_places = er_sb[:].rearrange("p (m j) -> p m j", m=P)
-        for n, tag in enumerate(("k0", "k1", "spread0", "spread1")):
-            er_wide = psum.tile([P, BLOCKS, P], F32, name=f"er_wide{n}", tag=tag)
-            for b in range(BLOCKS):
-                column = BLOCKS * n + b
-                nc.tensor.transpose(er_wide[:, b, :], er_upright[:, column : column + 1].to_broadcast([P, P]), identity[:])
-            nc.scalar.activation(out=er_places[:, :, BLOCKS * n : BLOCKS * (n + 1)], in_=er_wide[:].rearrange("p b m -> p m b"), func=COPY)
-
-        halves = [slice(h * HALF, (h + 1) * HALF) for h in range(2)]
-        x_listed = keep.tile([P, LANES - 1, SLOTS], BF16, name="x_listed")
-        x_grouped = keep.tile([P, SLOTS, LANES], BF16, name="x_grouped", align_bytes=64)
-        for t in range(LANES - 1):
-            nc.vector.tensor_copy(out=x_listed[:, t, :], in_=xT_sb[t][:].indirect(offsets[:]))
-        nc.vector.tensor_copy(
-            out=x_grouped[:, :, : LANES - 1].rearrange("p (c i) t -> p c t i", i=4), in_=x_listed[:].rearrange("p t (c i) -> p c t i", i=4)
-        )
-        for h in range(2):
-            nc.vector.tensor_copy(out=x_grouped[:, halves[h], LANES - 1], in_=xT_sb[LANES - 1][:].indirect(half_offsets[h]))
-        xE_sb = [keep.tile([P, TABLE], F32, name=f"xE{t}", tag=f"table{t}") for t in range(LANES)]
+        xE_sb = [keep.tile([P, TABLE], F32, name=f"xE{t}") for t in range(LANES)]
         for t in range(LANES):
             nc.sync.dma_start(xE_sb[t][:], xE_rows[:, t, :])
+
+        windows = [keep.tile([P, TABLE], F32, name=f"window{t}") for t in range(LANES)]
+        identity = keep.tile([P, P], F32, name="identity")
+        for t in range(2):
+            nc.vector.memset(windows[t][:], 0.0)
+        make_identity(nc, identity[:])
+        for t in range(2, LANES):
+            nc.gpsimd.memset(windows[t][:], 0.0)
+
+        er_sb = keep.tile([P, TABLE], F32, name="er_sb", tag="er_sb", align_bytes=64)
+        er_places = er_sb[:].rearrange("p (m j) -> p m j", m=P)
+        for n, tag in enumerate(("k0", "k1", "spare0", "spare1")):
+            er_wide = psum.tile([P, 4, P], F32, name=f"er_wide{n}", tag=tag)
+            for b in range(4):
+                column = 4 * n + b
+                nc.tensor.transpose(er_wide[:, b, :], er_upright[:, column : column + 1].to_broadcast([P, P]), identity[:])
+            nc.scalar.activation(out=er_places[:, :, 4 * n : 4 * (n + 1)], in_=er_wide[:].rearrange("p b m -> p m b"), func=COPY)
+
+        x_early = keep.tile([P, 2, SLOTS], F32, name="x_early", tag="x_early", align_bytes=64)
+        for v in range(2):
+            nc.vector.tensor_copy(out=x_early[:, v, :], in_=listed(xT_sb[0][:, v, :], every))
+        er_listed = keep.tile([P, SLOTS], F32, name="er_listed")
+        nc.vector.tensor_copy(out=er_listed[:], in_=listed(er_sb[:], every))
+        x_grouped = keep.tile([P, SLOTS, LANES], BF16, name="x_grouped", tag="er_sb", align_bytes=64)
         x_codes = keep.tile([P, SLOTS], U32, name="x_codes", align_bytes=64)
         x_scales = keep.tile([P, SLOTS], U8, name="x_scales", align_bytes=64)
-        for cols in halves:
-            nc.vector.quantize_mx(out=x_codes[:, cols].bitcast(FP8X4), scales=x_scales[:, cols], in_=x_grouped[:, cols, :].rearrange("p c t -> p (c t)"))
+        nc.scalar.copy(out=x_grouped[:, :, :2].rearrange("p (c i) t -> p c t i", i=4), in_=x_early[:].rearrange("p t (c i) -> p c t i", i=4))
+        for slots in halves:
+            for v in range(2):
+                nc.vector.tensor_copy(out=x_grouped[:, slots, 2 + v], in_=listed(xT_sb[1][:, v, :], slots))
 
-        pc_grouped = keep.tile([P, LANES, P, LANES], BF16, name="pc_grouped", tag="pc_grouped", align_bytes=64)
+        def quantise_x(slots):
+            nc.vector.quantize_mx(
+                out=x_codes[:, slots].bitcast(FP8X4), scales=x_scales[:, slots], in_=x_grouped[:, slots, :].rearrange("p c t -> p (c t)")
+            )
+
+        quantise_x(halves[0])
+
+        pc_grouped = keep.tile([P, LANES, P, LANES], BF16, name="pc_grouped", tag="x_early", align_bytes=64)
         dealt = pc_grouped[:].rearrange("p t m j -> p m j t")
         source = pc_sb[:].rearrange("p j (m t) -> p m j t", t=LANES)
         nc.scalar.copy(out=dealt[:, :SCALAR_DEAL], in_=source[:, :SCALAR_DEAL])
         nc.vector.tensor_copy(out=dealt[:, SCALAR_DEAL:], in_=source[:, SCALAR_DEAL:])
+        quantise_x(halves[1])
         pc_codes = keep.tile([P, SLOTS], U32, name="pc_codes", align_bytes=64)
         pc_scales = keep.tile([P, SLOTS], U8, name="pc_scales", align_bytes=64)
         for first, end in ((0, 1), (1, 2), (2, LANES)):
@@ -104,18 +115,14 @@ def tile_attend_grls_pl_kernel(tc, Pc, xT, xE, er, offs, out_0, out_1, out_2):
                 out=pc_codes[:, cols].bitcast(FP8X4), scales=pc_scales[:, cols], in_=pc_grouped[:, first:end].rearrange("p t m j -> p (t m j)")
             )
 
-        er_second = keep.tile([P, HALF], F32, name="er_second", tag="pc_grouped", align_bytes=64)
-        nc.vector.tensor_copy(out=er_second[:], in_=er_sb[:].indirect(half_offsets[1]))
-
         k_sb = [keep.tile([P, SLOTS], F32, name=f"k{t}") for t in range(LANES)]
-        pieces = [(0, halves[0], "k0"), (0, halves[1], "spread1")] + [(t, slice(0, SLOTS), f"k{t % 2}") for t in range(1, LANES)]
+        pieces = [(0, halves[0], "k0"), (0, halves[1], "spare1")] + [(t, every, f"k{t % 2}") for t in range(1, LANES)]
         for n, (t, slots, tag) in enumerate(pieces):
             k_bank = psum.tile([P, slots.stop - slots.start], F32, name=f"k_bank{n}", tag=tag)
-            cols = slice(t * P, (t + 1) * P)
             nc.tensor.matmul_mx(
                 out=k_bank[:],
-                lhsT=pc_codes[:, cols].bitcast(FP8X4),
-                lhsT_scale=pc_scales[:, cols],
+                lhsT=pc_codes[:, runs[t]].bitcast(FP8X4),
+                lhsT_scale=pc_scales[:, runs[t]],
                 rhs=x_codes[:, slots].bitcast(FP8X4),
                 rhs_scale=x_scales[:, slots],
                 start=True,
@@ -123,55 +130,43 @@ def tile_attend_grls_pl_kernel(tc, Pc, xT, xE, er, offs, out_0, out_1, out_2):
             )
             nc.scalar.copy(out=k_sb[t][:, slots], in_=k_bank[:])
 
-        er_turned = psum.tile([P, 2, P], F32, name="er_turned", tag="spread0")
+        er_turned = psum.tile([P, 2, P], F32, name="er_turned", tag="spare0")
         for i in range(2):
-            nc.tensor.transpose(er_turned[:, i, :], er_second[:, i * P : (i + 1) * P], identity[:])
+            nc.tensor.transpose(er_turned[:, i, :], er_listed[:, runs[2 + i]], identity[:])
         er_columns = keep.tile([P, 2], F32, name="er_columns")
         nc.scalar.copy(out=er_columns[:], in_=er_turned[:, :, 0])
 
-        sums = [psum.tile([P, P], F32, name=f"sums{b}", tag=f"sums{b}") for b in range(BLOCKS)]
-        for b in range(BLOCKS):
+        sums = [psum.tile([P, P], F32, name=f"sums{b}", tag=f"sums{b}") for b in range(RUNS)]
+        for b in range(RUNS):
             nc.tensor.matmul(sums[b][:], identity[:], identity[:], start=True, stop=False, is_transpose=True)
-        for t in range(LANES):
-            last = t == LANES - 1
+        for t, cuts in enumerate((halves, [every], [every], runs)):
             q = keep.tile([P, SLOTS], F32, name=f"q{t}")
-            if last:
-                for first, end in ((b * P, (b + 1) * P) for b in range(BLOCKS)):
-                    piece = offsets[:, first // 16 : end // 16]
-                    nc.vector.tensor_tensor(q[:, first:end], xE_sb[t][:].indirect(piece), k_sb[t][:, first:end], MULT)
-            elif t == 0:
-                for h in range(2):
-                    nc.vector.tensor_tensor(q[:, halves[h]], xE_sb[t][:].indirect(half_offsets[h]), k_sb[t][:, halves[h]], MULT)
-            else:
-                nc.vector.tensor_tensor(q[:], xE_sb[t][:].indirect(offsets[:]), k_sb[t][:], MULT)
-            if t == 1:
-                er_first = keep.tile([P, HALF], F32, name="er_first", tag="table1")
-                nc.vector.tensor_copy(out=er_first[:], in_=er_sb[:].indirect(half_offsets[0]))
-            for b in range(BLOCKS):
-                nc.tensor.matmul(sums[b][:], q[:, b * P : (b + 1) * P], identity[:], start=False, stop=last, is_transpose=True)
+            for slots in cuts:
+                nc.vector.tensor_tensor(q[:, slots], listed(xE_sb[t][:], slots), k_sb[t][:, slots], MULT)
+            for b in range(RUNS):
+                nc.tensor.matmul(sums[b][:], q[:, runs[b]], identity[:], start=False, stop=t == LANES - 1, is_transpose=True)
 
         factor = keep.tile([P, SLOTS], F32, name="factor")
-        summed = keep.tile([P, BLOCKS, P], F32, name="summed")
+        summed = keep.tile([P, RUNS, P], F32, name="summed")
         for b in range(2):
-            cols = slice(b * P, (b + 1) * P)
             denominator = keep.tile([P, 1], F32, name=f"denominator{b}")
             nc.scalar.activation(out=summed[:, b, :], in_=sums[b][:], func=COPY, accum_out=denominator[:])
             inverse = keep.tile([P, 1], F32, name=f"inverse{b}")
             nc.vector.reciprocal(out=inverse[:], in_=denominator[:])
             spread = psum.tile([P, P], F32, name=f"spread{b}", tag=f"k{b}")
             nc.tensor.transpose(spread[:], inverse[:].to_broadcast([P, P]), identity[:])
-            nc.vector.tensor_tensor(factor[:, cols], spread[:], er_first[:, cols], MULT)
+            nc.vector.tensor_tensor(factor[:, runs[b]], spread[:], er_listed[:, runs[b]], MULT)
         late_denominator = keep.tile([P, 2], F32, name="late_denominator")
         for i in range(2):
             nc.scalar.activation(out=summed[:, 2 + i, :], in_=sums[2 + i][:], func=COPY, accum_out=late_denominator[:, i : i + 1])
-        late_spread = psum.tile([P, 2, P], F32, name="late_spread", tag="spread1")
+        late_spread = psum.tile([P, 2, P], F32, name="late_spread", tag="spare1")
         late_inverse = keep.tile([P, 2], F32, name="late_inverse")
         nc.vector.reciprocal(out=late_inverse[:], in_=late_denominator[:])
         factor_columns = keep.tile([P, 2], F32, name="factor_columns")
         for i in range(2):
             nc.scalar.activation(out=factor_columns[:, i : i + 1], in_=late_inverse[:, i : i + 1], func=COPY, scale=er_columns[:, i : i + 1])
             nc.tensor.transpose(late_spread[:, i, :], factor_columns[:, i : i + 1].to_broadcast([P, P]), identity[:])
-        nc.scalar.copy(out=factor[:, HALF:], in_=late_spread[:].rearrange("p i m -> p (i m)"))
+        nc.scalar.copy(out=factor[:, halves[1]], in_=late_spread[:].rearrange("p i m -> p (i m)"))
 
         pairs = keep.tile([P, UNITS, 2, UNIT, 2], BF16, name="pairs")
 
@@ -181,12 +176,8 @@ def tile_attend_grls_pl_kernel(tc, Pc, xT, xE, er, offs, out_0, out_1, out_2):
             copy_on(nc, engine, target, source)
 
         for t in range(LANES):
-            if t == 0:
-                for h in range(2):
-                    cols = slice(h * HALF, (h + 1) * HALF)
-                    nc.vector.tensor_tensor(windows[t][:].indirect(half_offsets[h]), k_sb[t][:, cols], factor[:, cols], MULT)
-            else:
-                nc.vector.tensor_tensor(windows[t][:].indirect(offsets[:]), k_sb[t][:], factor[:], MULT)
+            for slots in halves if t == 0 else [every]:
+                nc.vector.tensor_tensor(listed(windows[t][:], slots), k_sb[t][:, slots], factor[:, slots], MULT)
             nc.sync.dma_start(out_rows[:, t, :], windows[t][:])
             if t < 2:
                 write_lane("scalar", t, 0, UNITS)

@@ -84,7 +84,7 @@ def tile_attend_grls_pl_kernel(tc, Pc, xT, xE, er, offs, out_0, out_1, out_2):
         x_early = keep.tile([P, 2, SLOTS], F32, name="x_early", tag="x_early", align_bytes=64)
         for v in range(2):
             nc.vector.tensor_copy(out=x_early[:, v, :], in_=listed(xT_sb[0][:, v, :], every))
-        er_listed = keep.tile([P, SLOTS], F32, name="er_listed")
+        er_listed = keep.tile([P, SLOTS], F32, name="er_listed", tag="er_listed")
         nc.vector.tensor_copy(out=er_listed[:], in_=listed(er_sb[:], every))
         x_grouped = keep.tile([P, SLOTS, LANES], BF16, name="x_grouped", tag="er_sb", align_bytes=64)
         x_codes = keep.tile([P, SLOTS], U32, name="x_codes", align_bytes=64)
@@ -130,24 +130,23 @@ def tile_attend_grls_pl_kernel(tc, Pc, xT, xE, er, offs, out_0, out_1, out_2):
             )
             nc.scalar.copy(out=k_sb[t][:, slots], in_=k_bank[:])
 
-        er_turned = psum.tile([P, 2, P], F32, name="er_turned", tag="spare0")
-        for i in range(2):
-            nc.tensor.transpose(er_turned[:, i, :], er_listed[:, runs[2 + i]], identity[:])
-        er_columns = keep.tile([P, 2], F32, name="er_columns")
-        nc.scalar.copy(out=er_columns[:], in_=er_turned[:, :, 0])
-
         sums = [psum.tile([P, P], F32, name=f"sums{b}", tag=f"sums{b}") for b in range(RUNS)]
         for b in range(RUNS):
             nc.tensor.matmul(sums[b][:], identity[:], identity[:], start=True, stop=False, is_transpose=True)
+        k_er = keep.tile([P, SLOTS], F32, name="k_er", tag="k_er")
         for t, cuts in enumerate((halves, [every], [every], runs)):
             q = keep.tile([P, SLOTS], F32, name=f"q{t}")
             for slots in cuts:
                 nc.vector.tensor_tensor(q[:, slots], listed(xE_sb[t][:], slots), k_sb[t][:, slots], MULT)
             for b in range(RUNS):
                 nc.tensor.matmul(sums[b][:], q[:, runs[b]], identity[:], start=False, stop=t == LANES - 1, is_transpose=True)
+            if t == 1:
+                nc.vector.tensor_tensor(k_er[:], k_sb[0][:], er_listed[:], MULT)
 
         factor = keep.tile([P, SLOTS], F32, name="factor")
         summed = keep.tile([P, RUNS, P], F32, name="summed")
+        up = {0: keep.tile([P, SLOTS], F32, name="up0")}
+        spreads = []
         for b in range(2):
             denominator = keep.tile([P, 1], F32, name=f"denominator{b}")
             nc.scalar.activation(out=summed[:, b, :], in_=sums[b][:], func=COPY, accum_out=denominator[:])
@@ -155,35 +154,55 @@ def tile_attend_grls_pl_kernel(tc, Pc, xT, xE, er, offs, out_0, out_1, out_2):
             nc.vector.reciprocal(out=inverse[:], in_=denominator[:])
             spread = psum.tile([P, P], F32, name=f"spread{b}", tag=f"k{b}")
             nc.tensor.transpose(spread[:], inverse[:].to_broadcast([P, P]), identity[:])
-            nc.vector.tensor_tensor(factor[:, runs[b]], spread[:], er_listed[:, runs[b]], MULT)
+            nc.vector.tensor_tensor(up[0][:, runs[b]], spread[:], k_er[:, runs[b]], MULT)
+            spreads.append(spread)
         late_denominator = keep.tile([P, 2], F32, name="late_denominator")
         for i in range(2):
             nc.scalar.activation(out=summed[:, 2 + i, :], in_=sums[2 + i][:], func=COPY, accum_out=late_denominator[:, i : i + 1])
         late_spread = psum.tile([P, 2, P], F32, name="late_spread", tag="spare1")
         late_inverse = keep.tile([P, 2], F32, name="late_inverse")
         nc.vector.reciprocal(out=late_inverse[:], in_=late_denominator[:])
-        factor_columns = keep.tile([P, 2], F32, name="factor_columns")
         for i in range(2):
-            nc.scalar.activation(out=factor_columns[:, i : i + 1], in_=late_inverse[:, i : i + 1], func=COPY, scale=er_columns[:, i : i + 1])
-            nc.tensor.transpose(late_spread[:, i, :], factor_columns[:, i : i + 1].to_broadcast([P, P]), identity[:])
-        nc.scalar.copy(out=factor[:, halves[1]], in_=late_spread[:].rearrange("p i m -> p (i m)"))
+            nc.tensor.transpose(late_spread[:, i, :], late_inverse[:, i : i + 1].to_broadcast([P, P]), identity[:])
+        late_flat = late_spread[:].rearrange("p i m -> p (i m)")
+        for b in range(2):
+            nc.vector.tensor_tensor(factor[:, runs[b]], spreads[b][:], er_listed[:, runs[b]], MULT)
+        nc.vector.tensor_tensor(up[0][:, halves[1]], late_flat, k_er[:, halves[1]], MULT)
+        nc.vector.tensor_tensor(factor[:, halves[1]], late_flat, er_listed[:, halves[1]], MULT)
+
+        up[2] = keep.tile([P, SLOTS], F32, name="up2", tag="k_er")
+        up[3] = keep.tile([P, SLOTS], F32, name="up3", tag="er_listed")
+
+        def product(t, slots):
+            nc.vector.tensor_tensor(up[t][:, slots], k_sb[t][:, slots], factor[:, slots], MULT)
+
+        def scatter_on_scalar(t, slots):
+            nc.scalar.activation(out=listed(windows[t][:], slots), in_=up[t][:, slots], func=COPY)
+
+        def store_lane(t):
+            nc.sync.dma_start(out_rows[:, t, :], windows[t][:])
 
         pairs = keep.tile([P, UNITS, 2, UNIT, 2], BF16, name="pairs")
 
-        def write_lane(engine, t, first, last):
+        def write_lane(t, first, last):
             source = windows[t][:, first * UNIT : last * UNIT].rearrange("p (n h c) -> p h n c", h=2, c=UNIT // 2)
             target = pairs[:, first:last, t // 2, :, t % 2].rearrange("p n (h c) -> p h n c", h=2)
-            copy_on(nc, engine, target, source)
+            nc.vector.tensor_copy(out=target, in_=source)
 
-        for t in range(LANES):
-            for slots in halves if t == 0 else [every]:
-                nc.vector.tensor_tensor(listed(windows[t][:], slots), k_sb[t][:, slots], factor[:, slots], MULT)
-            nc.sync.dma_start(out_rows[:, t, :], windows[t][:])
-            if t < 2:
-                write_lane("scalar", t, 0, UNITS)
-            if t == 2:
-                write_lane("scalar", t, 0, 1)
-                write_lane("scalar", t, 4, UNITS)
+        for slots in halves:
+            scatter_on_scalar(0, slots)
+        store_lane(0)
+        for t in (2, 3):
+            product(t, halves[0])
+            scatter_on_scalar(t, halves[0])
+        nc.vector.tensor_tensor(listed(windows[1][:], every), k_sb[1][:], factor[:], MULT)
+        store_lane(1)
+        for t in (2, 3):
+            product(t, halves[1])
+            scatter_on_scalar(t, halves[1])
+            store_lane(t)
+        for t in range(3):
+            write_lane(t, 0, UNITS)
 
         words_out = out_1[0].rearrange("p c l -> p (c l)").bitcast(I32)
         out_scales = keep.tile([P, PLANE], U8, name="out_scales", align_bytes=64)
@@ -209,31 +228,17 @@ def tile_attend_grls_pl_kernel(tc, Pc, xT, xE, er, offs, out_0, out_1, out_2):
             cols = slice(first * UNIT, last * UNIT)
             nc.sync.dma_start(words_out[:, cols], codes[:, cols].bitcast(I32))
 
-        write_lane("vector", 2, 1, 4)
-        write_lane("vector", 3, 1, 2)
-        write_lane("vector", 3, 2, 4)
-        for first, last in ((0, 1), (4, 5), (5, 8), (8, 12), (12, 16)):
-            write_lane("scalar", 3, first, last)
-        for first, last in ((10, 12), (12, 14), (14, 15)):
-            merge("scalar", first, last)
-        merge("vector", 0, 2)
-        merge("vector", 2, 5)
-        quantise(0, 2)
-        merge("vector", 5, 8)
-        quantise(2, 4)
-        store(0, 4)
-        merge("vector", 8, 10)
-        quantise(4, 6)
-        quantise(6, 8)
-        store(4, 8)
-        merge("vector", 15, 16)
-        quantise(8, 10)
-        quantise(10, 12)
-        store(8, 12)
+        for first, last in ((0, 2), (2, 8), (8, 16)):
+            write_lane(3, first, last)
+        for first in (0, 2, 8, 10, 12, 14):
+            merge("scalar", first, first + 2)
+        merge("vector", 4, 8)
+        for first in (0, 4, 8):
+            quantise(first, first + 4)
+            store(first, first + 4)
         quantise(12, 14)
-        store(12, 14)
         quantise(14, 16)
-        store(14, 16)
+        store(12, 16)
         scales_out = out_2[0].bitcast(I32).rearrange("r (j c) -> j r c", j=4)
         for quadrant in range(4):
             queue = nc.sync if quadrant % 2 == 0 else nc.scalar

@@ -133,30 +133,30 @@ def tile_attend_grls_pl_kernel(tc, Pc, xT, xE, er, offs, out_0, out_1, out_2):
         sums = [psum.tile([P, P], F32, name=f"sums{b}", tag=f"sums{b}") for b in range(RUNS)]
         for b in range(RUNS):
             nc.tensor.matmul(sums[b][:], identity[:], identity[:], start=True, stop=False, is_transpose=True)
-        k_er = keep.tile([P, SLOTS], F32, name="k_er", tag="k_er")
         for t, cuts in enumerate((halves, [every], [every], runs)):
             q = keep.tile([P, SLOTS], F32, name=f"q{t}")
             for slots in cuts:
                 nc.vector.tensor_tensor(q[:, slots], listed(xE_sb[t][:], slots), k_sb[t][:, slots], MULT)
             for b in range(RUNS):
                 nc.tensor.matmul(sums[b][:], q[:, runs[b]], identity[:], start=False, stop=t == LANES - 1, is_transpose=True)
-            if t == 1:
-                nc.vector.tensor_tensor(k_er[:], k_sb[0][:], er_listed[:], MULT)
 
         factor = keep.tile([P, SLOTS], F32, name="factor")
         summed = keep.tile([P, RUNS, P], F32, name="summed")
         up = {0: keep.tile([P, SLOTS], F32, name="up0")}
         spreads = []
         for b in range(2):
-            denominator = keep.tile([P, 1], F32, name=f"denominator{b}")
+            denominator = keep.tile([P, 1], F32, name=f"denominator{b}", tag=f"early{b}")
             nc.scalar.activation(out=summed[:, b, :], in_=sums[b][:], func=COPY, accum_out=denominator[:])
             inverse = keep.tile([P, 1], F32, name=f"inverse{b}")
             nc.vector.reciprocal(out=inverse[:], in_=denominator[:])
             spread = psum.tile([P, P], F32, name=f"spread{b}", tag=f"k{b}")
             nc.tensor.transpose(spread[:], inverse[:].to_broadcast([P, P]), identity[:])
-            nc.vector.tensor_tensor(up[0][:, runs[b]], spread[:], k_er[:, runs[b]], MULT)
             spreads.append(spread)
-        late_denominator = keep.tile([P, 2], F32, name="late_denominator")
+        k_er_early = keep.tile([P, HALF], F32, name="k_er_early", tag="early1")
+        nc.vector.tensor_tensor(k_er_early[:], k_sb[0][:, halves[0]], er_listed[:, halves[0]], MULT)
+        for b in range(2):
+            nc.vector.tensor_tensor(up[0][:, runs[b]], spreads[b][:], k_er_early[:, runs[b]], MULT)
+        late_denominator = keep.tile([P, 2], F32, name="late_denominator", tag="late")
         for i in range(2):
             nc.scalar.activation(out=summed[:, 2 + i, :], in_=sums[2 + i][:], func=COPY, accum_out=late_denominator[:, i : i + 1])
         late_spread = psum.tile([P, 2, P], F32, name="late_spread", tag="spare1")
@@ -165,12 +165,14 @@ def tile_attend_grls_pl_kernel(tc, Pc, xT, xE, er, offs, out_0, out_1, out_2):
         for i in range(2):
             nc.tensor.transpose(late_spread[:, i, :], late_inverse[:, i : i + 1].to_broadcast([P, P]), identity[:])
         late_flat = late_spread[:].rearrange("p i m -> p (i m)")
+        k_er_late = keep.tile([P, HALF], F32, name="k_er_late", tag="late")
+        nc.vector.tensor_tensor(k_er_late[:], k_sb[0][:, halves[1]], er_listed[:, halves[1]], MULT)
         for b in range(2):
             nc.vector.tensor_tensor(factor[:, runs[b]], spreads[b][:], er_listed[:, runs[b]], MULT)
-        nc.vector.tensor_tensor(up[0][:, halves[1]], late_flat, k_er[:, halves[1]], MULT)
+        nc.vector.tensor_tensor(up[0][:, halves[1]], late_flat, k_er_late[:], MULT)
         nc.vector.tensor_tensor(factor[:, halves[1]], late_flat, er_listed[:, halves[1]], MULT)
 
-        up[2] = keep.tile([P, SLOTS], F32, name="up2", tag="k_er")
+        up[2] = keep.tile([P, SLOTS], F32, name="up2", tag="late")
         up[3] = keep.tile([P, SLOTS], F32, name="up3", tag="er_listed")
 
         def product(t, slots):

@@ -22,8 +22,10 @@ RUNS = SLOTS // P
 FLOPS = 2 * 512 * 512 * 512
 
 SCALAR_DEAL = 72
+HELD = 16
 UNIT = 128
 UNITS = TABLE // UNIT
+SCALAR_UNITS = 2
 PLANE = TABLE // 4
 
 
@@ -84,8 +86,9 @@ def tile_attend_grls_pl_kernel(tc, Pc, xT, xE, er, offs, out_0, out_1, out_2):
         x_early = keep.tile([P, 2, SLOTS], F32, name="x_early", tag="x_early", align_bytes=64)
         for v in range(2):
             nc.vector.tensor_copy(out=x_early[:, v, :], in_=listed(xT_sb[0][:, v, :], every))
-        er_listed = keep.tile([P, SLOTS], F32, name="er_listed", tag="er_listed")
-        nc.vector.tensor_copy(out=er_listed[:], in_=listed(er_sb[:], every))
+        er_then_up3 = keep.tile([P, SLOTS + HELD], F32, name="er_then_up3")
+        er_listed = er_then_up3[:, :SLOTS]
+        nc.vector.tensor_copy(out=er_listed, in_=listed(er_sb[:], every))
         x_grouped = keep.tile([P, SLOTS, LANES], BF16, name="x_grouped", tag="er_sb", align_bytes=64)
         x_codes = keep.tile([P, SLOTS], U32, name="x_codes", align_bytes=64)
         x_scales = keep.tile([P, SLOTS], U8, name="x_scales", align_bytes=64)
@@ -115,7 +118,7 @@ def tile_attend_grls_pl_kernel(tc, Pc, xT, xE, er, offs, out_0, out_1, out_2):
                 out=pc_codes[:, cols].bitcast(FP8X4), scales=pc_scales[:, cols], in_=pc_grouped[:, first:end].rearrange("p t m j -> p (t m j)")
             )
 
-        k_sb = [keep.tile([P, SLOTS], F32, name=f"k{t}") for t in range(LANES)]
+        k_sb = [keep.tile([P, SLOTS], F32, name=f"k{t}", tag=f"k_lane{t}") for t in range(LANES)]
         pieces = [(0, halves[0], "k0"), (0, halves[1], "spare1")] + [(t, every, f"k{t % 2}") for t in range(1, LANES)]
         for n, (t, slots, tag) in enumerate(pieces):
             k_bank = psum.tile([P, slots.stop - slots.start], F32, name=f"k_bank{n}", tag=tag)
@@ -140,10 +143,11 @@ def tile_attend_grls_pl_kernel(tc, Pc, xT, xE, er, offs, out_0, out_1, out_2):
             for b in range(RUNS):
                 nc.tensor.matmul(sums[b][:], q[:, runs[b]], identity[:], start=False, stop=t == LANES - 1, is_transpose=True)
 
-        factor = keep.tile([P, SLOTS], F32, name="factor")
+        factor = keep.tile([P, SLOTS], F32, name="factor", tag="factor")
         summed = keep.tile([P, RUNS, P], F32, name="summed")
         up = {0: keep.tile([P, SLOTS], F32, name="up0")}
         spreads = []
+        k_er_early = []
         for b in range(2):
             denominator = keep.tile([P, 1], F32, name=f"denominator{b}", tag=f"early{b}")
             nc.scalar.activation(out=summed[:, b, :], in_=sums[b][:], func=COPY, accum_out=denominator[:])
@@ -152,10 +156,10 @@ def tile_attend_grls_pl_kernel(tc, Pc, xT, xE, er, offs, out_0, out_1, out_2):
             spread = psum.tile([P, P], F32, name=f"spread{b}", tag=f"k{b}")
             nc.tensor.transpose(spread[:], inverse[:].to_broadcast([P, P]), identity[:])
             spreads.append(spread)
-        k_er_early = keep.tile([P, HALF], F32, name="k_er_early", tag="early1")
-        nc.vector.tensor_tensor(k_er_early[:], k_sb[0][:, halves[0]], er_listed[:, halves[0]], MULT)
+            k_er_early.append(keep.tile([P, P], F32, name=f"k_er_early{b}", tag=f"early{b}"))
+            nc.vector.tensor_tensor(k_er_early[b][:], k_sb[0][:, runs[b]], er_listed[:, runs[b]], MULT)
         for b in range(2):
-            nc.vector.tensor_tensor(up[0][:, runs[b]], spreads[b][:], k_er_early[:, runs[b]], MULT)
+            nc.vector.tensor_tensor(up[0][:, runs[b]], spreads[b][:], k_er_early[b][:], MULT)
         late_denominator = keep.tile([P, 2], F32, name="late_denominator", tag="late")
         for i in range(2):
             nc.scalar.activation(out=summed[:, 2 + i, :], in_=sums[2 + i][:], func=COPY, accum_out=late_denominator[:, i : i + 1])
@@ -165,18 +169,20 @@ def tile_attend_grls_pl_kernel(tc, Pc, xT, xE, er, offs, out_0, out_1, out_2):
         for i in range(2):
             nc.tensor.transpose(late_spread[:, i, :], late_inverse[:, i : i + 1].to_broadcast([P, P]), identity[:])
         late_flat = late_spread[:].rearrange("p i m -> p (i m)")
-        k_er_late = keep.tile([P, HALF], F32, name="k_er_late", tag="late")
-        nc.vector.tensor_tensor(k_er_late[:], k_sb[0][:, halves[1]], er_listed[:, halves[1]], MULT)
+        up[2] = keep.tile([P, SLOTS], F32, name="up2", tag="late")
+        up[3] = er_then_up3[:, HELD:]
+        k_er_late = up[2][:, HALF - HELD : SLOTS - HELD]
+        nc.vector.tensor_tensor(k_er_late, k_sb[0][:, halves[1]], er_listed[:, halves[1]], MULT)
         for b in range(2):
             nc.vector.tensor_tensor(factor[:, runs[b]], spreads[b][:], er_listed[:, runs[b]], MULT)
-        nc.vector.tensor_tensor(up[0][:, halves[1]], late_flat, k_er_late[:], MULT)
-        nc.vector.tensor_tensor(factor[:, halves[1]], late_flat, er_listed[:, halves[1]], MULT)
-
-        up[2] = keep.tile([P, SLOTS], F32, name="up2", tag="late")
-        up[3] = keep.tile([P, SLOTS], F32, name="up3", tag="er_listed")
 
         def product(t, slots):
             nc.vector.tensor_tensor(up[t][:, slots], k_sb[t][:, slots], factor[:, slots], MULT)
+
+        for t in (2, 3):
+            product(t, slice(0, HALF - HELD))
+        nc.vector.tensor_tensor(up[0][:, halves[1]], late_flat, k_er_late, MULT)
+        nc.vector.tensor_tensor(factor[:, halves[1]], late_flat, er_listed[:, halves[1]], MULT)
 
         def scatter_on_scalar(t, slots):
             nc.scalar.activation(out=listed(windows[t][:], slots), in_=up[t][:, slots], func=COPY)
@@ -184,18 +190,24 @@ def tile_attend_grls_pl_kernel(tc, Pc, xT, xE, er, offs, out_0, out_1, out_2):
         def store_lane(t):
             nc.sync.dma_start(out_rows[:, t, :], windows[t][:])
 
-        pairs = keep.tile([P, UNITS, 2, UNIT, 2], BF16, name="pairs")
+        vector_pairs = keep.tile([P, UNITS - SCALAR_UNITS, 2, UNIT, 2], BF16, name="vector_pairs", tag="factor")
+        scalar_pairs = keep.tile([P, SCALAR_UNITS, 2, UNIT, 2], BF16, name="scalar_pairs", tag="k_lane1")
 
-        def write_lane(t, first, last):
+        def pairs(first, last):
+            if first < SCALAR_UNITS:
+                return scalar_pairs[:, first:last]
+            return vector_pairs[:, first - SCALAR_UNITS : last - SCALAR_UNITS]
+
+        def write_lane(engine, t, first, last):
             source = windows[t][:, first * UNIT : last * UNIT].rearrange("p (n h c) -> p h n c", h=2, c=UNIT // 2)
-            target = pairs[:, first:last, t // 2, :, t % 2].rearrange("p n (h c) -> p h n c", h=2)
-            nc.vector.tensor_copy(out=target, in_=source)
+            target = pairs(first, last)[:, :, t // 2, :, t % 2].rearrange("p n (h c) -> p h n c", h=2)
+            copy_on(nc, engine, target, source)
 
         for slots in halves:
             scatter_on_scalar(0, slots)
         store_lane(0)
         for t in (2, 3):
-            product(t, halves[0])
+            product(t, slice(HALF - HELD, HALF))
             scatter_on_scalar(t, halves[0])
         nc.vector.tensor_tensor(listed(windows[1][:], every), k_sb[1][:], factor[:], MULT)
         store_lane(1)
@@ -204,7 +216,11 @@ def tile_attend_grls_pl_kernel(tc, Pc, xT, xE, er, offs, out_0, out_1, out_2):
             scatter_on_scalar(t, halves[1])
             store_lane(t)
         for t in range(3):
-            write_lane(t, 0, UNITS)
+            write_lane("vector", t, SCALAR_UNITS, UNITS)
+            if t < 2:
+                write_lane("vector", t, 0, SCALAR_UNITS)
+        for t in (2, 3):
+            write_lane("scalar", t, 0, SCALAR_UNITS)
 
         words_out = out_1[0].rearrange("p c l -> p (c l)").bitcast(I32)
         out_scales = keep.tile([P, PLANE], U8, name="out_scales", align_bytes=64)
@@ -213,7 +229,7 @@ def tile_attend_grls_pl_kernel(tc, Pc, xT, xE, er, offs, out_0, out_1, out_2):
 
         def merge(engine, first, last):
             word = U32 if engine == "scalar" else I32
-            source = pairs[:, first:last].rearrange("p n u c v -> p n u (c v)").bitcast(word).rearrange("p n u (h c) -> p h n c u", h=2)
+            source = pairs(first, last).rearrange("p n u c v -> p n u (c v)").bitcast(word).rearrange("p n u (h c) -> p h n c u", h=2)
             target = grouped[:, first * UNIT * LANES : last * UNIT * LANES]
             copy_on(nc, engine, target.bitcast(word).rearrange("p (n h c u) -> p h n c u", h=2, c=UNIT // 2, u=2), source)
 
@@ -230,17 +246,15 @@ def tile_attend_grls_pl_kernel(tc, Pc, xT, xE, er, offs, out_0, out_1, out_2):
             cols = slice(first * UNIT, last * UNIT)
             nc.sync.dma_start(words_out[:, cols], codes[:, cols].bitcast(I32))
 
-        for first, last in ((0, 2), (2, 8), (8, 16)):
-            write_lane(3, first, last)
+        for first, last in ((2, 4), (4, 10), (10, 16)):
+            write_lane("vector", 3, first, last)
         for first in (0, 2, 8, 10, 12, 14):
             merge("scalar", first, first + 2)
         merge("vector", 4, 8)
-        for first in (0, 4, 8):
-            quantise(first, first + 4)
+        for first in range(0, UNITS, 4):
+            quantise(first, first + 2)
+            quantise(first + 2, first + 4)
             store(first, first + 4)
-        quantise(12, 14)
-        quantise(14, 16)
-        store(12, 16)
         scales_out = out_2[0].bitcast(I32).rearrange("r (j c) -> j r c", j=4)
         for quadrant in range(4):
             queue = nc.sync if quadrant % 2 == 0 else nc.scalar

@@ -22,7 +22,6 @@ RUNS = SLOTS // P
 FLOPS = 2 * 512 * 512 * 512
 
 SCALAR_DEAL = 72
-HELD = 16
 UNIT = 128
 UNITS = TABLE // UNIT
 SCALAR_UNITS = 2
@@ -86,9 +85,8 @@ def tile_attend_grls_pl_kernel(tc, Pc, xT, xE, er, offs, out_0, out_1, out_2):
         x_early = keep.tile([P, 2, SLOTS], F32, name="x_early", tag="x_early", align_bytes=64)
         for v in range(2):
             nc.vector.tensor_copy(out=x_early[:, v, :], in_=listed(xT_sb[0][:, v, :], every))
-        er_then_up3 = keep.tile([P, SLOTS + HELD], F32, name="er_then_up3")
-        er_listed = er_then_up3[:, :SLOTS]
-        nc.vector.tensor_copy(out=er_listed, in_=listed(er_sb[:], every))
+        er_listed = keep.tile([P, SLOTS], F32, name="er_listed")
+        nc.vector.tensor_copy(out=er_listed[:], in_=listed(er_sb[:], every))
         x_grouped = keep.tile([P, SLOTS, LANES], BF16, name="x_grouped", tag="er_sb", align_bytes=64)
         x_codes = keep.tile([P, SLOTS], U32, name="x_codes", align_bytes=64)
         x_scales = keep.tile([P, SLOTS], U8, name="x_scales", align_bytes=64)
@@ -118,9 +116,17 @@ def tile_attend_grls_pl_kernel(tc, Pc, xT, xE, er, offs, out_0, out_1, out_2):
                 out=pc_codes[:, cols].bitcast(FP8X4), scales=pc_scales[:, cols], in_=pc_grouped[:, first:end].rearrange("p t m j -> p (t m j)")
             )
 
-        k_sb = [keep.tile([P, SLOTS], F32, name=f"k{t}", tag=f"k_lane{t}") for t in range(LANES)]
-        pieces = [(0, halves[0], "k0"), (0, halves[1], "spare1")] + [(t, every, f"k{t % 2}") for t in range(1, LANES)]
-        for n, (t, slots, tag) in enumerate(pieces):
+        k0 = keep.tile([P, SLOTS], F32, name="k0")
+        k1 = keep.tile([P, SLOTS], F32, name="k1", tag="k_lane1")
+        k_late = keep.tile([P, 2, SLOTS], F32, name="k_late")
+        pieces = (
+            (0, halves[0], "k0", k0[:, halves[0]]),
+            (0, halves[1], "spare1", k0[:, halves[1]]),
+            (1, every, "k1", k1[:]),
+            (2, every, "k0", k_late[:, 0, :]),
+            (3, every, "k1", k_late[:, 1, :]),
+        )
+        for n, (t, slots, tag, target) in enumerate(pieces):
             k_bank = psum.tile([P, slots.stop - slots.start], F32, name=f"k_bank{n}", tag=tag)
             nc.tensor.matmul_mx(
                 out=k_bank[:],
@@ -131,21 +137,27 @@ def tile_attend_grls_pl_kernel(tc, Pc, xT, xE, er, offs, out_0, out_1, out_2):
                 start=True,
                 stop=True,
             )
-            nc.scalar.copy(out=k_sb[t][:, slots], in_=k_bank[:])
+            nc.scalar.copy(out=target, in_=k_bank[:])
 
         sums = [psum.tile([P, P], F32, name=f"sums{b}", tag=f"sums{b}") for b in range(RUNS)]
         for b in range(RUNS):
             nc.tensor.matmul(sums[b][:], identity[:], identity[:], start=True, stop=False, is_transpose=True)
-        for t, cuts in enumerate((halves, [every], [every], runs)):
+        cuts = (
+            tuple((half, k0[:, half]) for half in halves),
+            ((every, k1[:]),),
+            ((every, k_late[:, 0, :]),),
+            tuple((run, k_late[:, 1, run]) for run in runs),
+        )
+        for t in range(LANES):
             q = keep.tile([P, SLOTS], F32, name=f"q{t}")
-            for slots in cuts:
-                nc.vector.tensor_tensor(q[:, slots], listed(xE_sb[t][:], slots), k_sb[t][:, slots], MULT)
+            for slots, k_piece in cuts[t]:
+                nc.vector.tensor_tensor(q[:, slots], listed(xE_sb[t][:], slots), k_piece, MULT)
             for b in range(RUNS):
                 nc.tensor.matmul(sums[b][:], q[:, runs[b]], identity[:], start=False, stop=t == LANES - 1, is_transpose=True)
 
         factor = keep.tile([P, SLOTS], F32, name="factor", tag="factor")
         summed = keep.tile([P, RUNS, P], F32, name="summed")
-        up = {0: keep.tile([P, SLOTS], F32, name="up0")}
+        up0 = keep.tile([P, SLOTS], F32, name="up0")
         spreads = []
         k_er_early = []
         for b in range(2):
@@ -157,10 +169,10 @@ def tile_attend_grls_pl_kernel(tc, Pc, xT, xE, er, offs, out_0, out_1, out_2):
             nc.tensor.transpose(spread[:], inverse[:].to_broadcast([P, P]), identity[:])
             spreads.append(spread)
             k_er_early.append(keep.tile([P, P], F32, name=f"k_er_early{b}", tag=f"early{b}"))
-            nc.vector.tensor_tensor(k_er_early[b][:], k_sb[0][:, runs[b]], er_listed[:, runs[b]], MULT)
+            nc.vector.tensor_tensor(k_er_early[b][:], k0[:, runs[b]], er_listed[:, runs[b]], MULT)
         for b in range(2):
-            nc.vector.tensor_tensor(up[0][:, runs[b]], spreads[b][:], k_er_early[b][:], MULT)
-        late_denominator = keep.tile([P, 2], F32, name="late_denominator", tag="late")
+            nc.vector.tensor_tensor(up0[:, runs[b]], spreads[b][:], k_er_early[b][:], MULT)
+        late_denominator = keep.tile([P, 2], F32, name="late_denominator")
         for i in range(2):
             nc.scalar.activation(out=summed[:, 2 + i, :], in_=sums[2 + i][:], func=COPY, accum_out=late_denominator[:, i : i + 1])
         late_spread = psum.tile([P, 2, P], F32, name="late_spread", tag="spare1")
@@ -169,23 +181,22 @@ def tile_attend_grls_pl_kernel(tc, Pc, xT, xE, er, offs, out_0, out_1, out_2):
         for i in range(2):
             nc.tensor.transpose(late_spread[:, i, :], late_inverse[:, i : i + 1].to_broadcast([P, P]), identity[:])
         late_flat = late_spread[:].rearrange("p i m -> p (i m)")
-        up[2] = keep.tile([P, SLOTS], F32, name="up2", tag="late")
-        up[3] = er_then_up3[:, HELD:]
-        k_er_late = up[2][:, HALF - HELD : SLOTS - HELD]
-        nc.vector.tensor_tensor(k_er_late, k_sb[0][:, halves[1]], er_listed[:, halves[1]], MULT)
         for b in range(2):
             nc.vector.tensor_tensor(factor[:, runs[b]], spreads[b][:], er_listed[:, runs[b]], MULT)
-
-        def product(t, slots):
-            nc.vector.tensor_tensor(up[t][:, slots], k_sb[t][:, slots], factor[:, slots], MULT)
-
-        for t in (2, 3):
-            product(t, slice(0, HALF - HELD))
-        nc.vector.tensor_tensor(up[0][:, halves[1]], late_flat, k_er_late, MULT)
         nc.vector.tensor_tensor(factor[:, halves[1]], late_flat, er_listed[:, halves[1]], MULT)
 
-        def scatter_on_scalar(t, slots):
-            nc.scalar.activation(out=listed(windows[t][:], slots), in_=up[t][:, slots], func=COPY)
+        up_late = [keep.tile([P, 2, HALF], F32, name=f"up_late{h}") for h in range(2)]
+
+        def late_product(h):
+            both = factor[:, halves[h]].unsqueeze(1).to_broadcast([P, 2, HALF])
+            nc.vector.tensor_tensor(up_late[h][:], k_late[:, :, halves[h]], both, MULT)
+
+        late_product(0)
+        nc.vector.tensor_tensor(up0[:, halves[1]], k0[:, halves[1]], factor[:, halves[1]], MULT)
+        late_product(1)
+
+        def scatter_on_scalar(t, slots, source):
+            nc.scalar.activation(out=listed(windows[t][:], slots), in_=source, func=COPY)
 
         def store_lane(t):
             nc.sync.dma_start(out_rows[:, t, :], windows[t][:])
@@ -204,16 +215,14 @@ def tile_attend_grls_pl_kernel(tc, Pc, xT, xE, er, offs, out_0, out_1, out_2):
             copy_on(nc, engine, target, source)
 
         for slots in halves:
-            scatter_on_scalar(0, slots)
+            scatter_on_scalar(0, slots, up0[:, slots])
         store_lane(0)
-        for t in (2, 3):
-            product(t, slice(HALF - HELD, HALF))
-            scatter_on_scalar(t, halves[0])
-        nc.vector.tensor_tensor(listed(windows[1][:], every), k_sb[1][:], factor[:], MULT)
+        nc.vector.tensor_tensor(listed(windows[1][:], every), k1[:], factor[:], MULT)
         store_lane(1)
+        for h in (1, 0):
+            for t in (2, 3):
+                scatter_on_scalar(t, halves[h], up_late[h][:, t - 2, :])
         for t in (2, 3):
-            product(t, halves[1])
-            scatter_on_scalar(t, halves[1])
             store_lane(t)
         for t in range(3):
             write_lane("vector", t, SCALAR_UNITS, UNITS)

@@ -185,15 +185,14 @@ def tile_attend_grls_pl_kernel(tc, Pc, xT, xE, er, offs, out_0, out_1, out_2):
             nc.vector.tensor_tensor(factor[:, runs[b]], spreads[b][:], er_listed[:, runs[b]], MULT)
         nc.vector.tensor_tensor(factor[:, halves[1]], late_flat, er_listed[:, halves[1]], MULT)
 
-        up_late = [keep.tile([P, 2, HALF], F32, name=f"up_late{h}") for h in range(2)]
-
-        def late_product(h):
-            both = factor[:, halves[h]].unsqueeze(1).to_broadcast([P, 2, HALF])
-            nc.vector.tensor_tensor(up_late[h][:], k_late[:, :, halves[h]], both, MULT)
-
-        late_product(0)
+        up1 = keep.tile([P, SLOTS], F32, name="up1", tag="up1")
+        nc.vector.tensor_tensor(up1[:, halves[0]], k1[:, halves[0]], factor[:, halves[0]], MULT)
         nc.vector.tensor_tensor(up0[:, halves[1]], k0[:, halves[1]], factor[:, halves[1]], MULT)
-        late_product(1)
+        nc.vector.tensor_tensor(up1[:, halves[1]], k1[:, halves[1]], factor[:, halves[1]], MULT)
+        up_late = keep.tile([P, 2, SLOTS], F32, name="up_late", tag="k_lane1")
+        for slots in halves:
+            both = factor[:, slots].unsqueeze(1).to_broadcast([P, 2, HALF])
+            nc.gpsimd.tensor_tensor(up_late[:, :, slots], k_late[:, :, slots], both, MULT)
 
         def scatter_on_scalar(t, slots, source):
             nc.scalar.activation(out=listed(windows[t][:], slots), in_=source, func=COPY)
@@ -202,7 +201,7 @@ def tile_attend_grls_pl_kernel(tc, Pc, xT, xE, er, offs, out_0, out_1, out_2):
             nc.sync.dma_start(out_rows[:, t, :], windows[t][:])
 
         vector_pairs = keep.tile([P, UNITS - SCALAR_UNITS, 2, UNIT, 2], BF16, name="vector_pairs", tag="factor")
-        scalar_pairs = keep.tile([P, SCALAR_UNITS, 2, UNIT, 2], BF16, name="scalar_pairs", tag="k_lane1")
+        scalar_pairs = keep.tile([P, SCALAR_UNITS, 2, UNIT, 2], BF16, name="scalar_pairs", tag="up1")
 
         def pairs(first, last):
             if first < SCALAR_UNITS:
@@ -217,11 +216,11 @@ def tile_attend_grls_pl_kernel(tc, Pc, xT, xE, er, offs, out_0, out_1, out_2):
         for slots in halves:
             scatter_on_scalar(0, slots, up0[:, slots])
         store_lane(0)
-        nc.vector.tensor_tensor(listed(windows[1][:], every), k1[:], factor[:], MULT)
+        nc.vector.tensor_copy(out=listed(windows[1][:], every), in_=up1[:])
         store_lane(1)
-        for h in (1, 0):
+        for slots in halves:
             for t in (2, 3):
-                scatter_on_scalar(t, halves[h], up_late[h][:, t - 2, :])
+                scatter_on_scalar(t, slots, up_late[:, t - 2, slots])
         for t in (2, 3):
             store_lane(t)
         for t in range(3):

@@ -116,13 +116,14 @@ def tile_attend_grls_pl_kernel(tc, Pc, xT, xE, er, offs, out_0, out_1, out_2):
                 out=pc_codes[:, cols].bitcast(FP8X4), scales=pc_scales[:, cols], in_=pc_grouped[:, first:end].rearrange("p t m j -> p (t m j)")
             )
 
-        k0 = keep.tile([P, SLOTS], F32, name="k0")
-        k1 = keep.tile([P, SLOTS], F32, name="k1", tag="k_lane1")
+        k_early = keep.tile([P, 2, SLOTS], F32, name="k_early", tag="k_early")
+        k0 = k_early[:, 0, :]
+        k1 = k_early[:, 1, :]
         k_late = keep.tile([P, 2, SLOTS], F32, name="k_late")
         pieces = (
             (0, halves[0], "k0", k0[:, halves[0]]),
             (0, halves[1], "spare1", k0[:, halves[1]]),
-            (1, every, "k1", k1[:]),
+            (1, every, "k1", k1),
             (2, every, "k0", k_late[:, 0, :]),
             (3, every, "k1", k_late[:, 1, :]),
         )
@@ -144,7 +145,7 @@ def tile_attend_grls_pl_kernel(tc, Pc, xT, xE, er, offs, out_0, out_1, out_2):
             nc.tensor.matmul(sums[b][:], identity[:], identity[:], start=True, stop=False, is_transpose=True)
         cuts = (
             tuple((half, k0[:, half]) for half in halves),
-            ((every, k1[:]),),
+            ((every, k1),),
             ((every, k_late[:, 0, :]),),
             tuple((run, k_late[:, 1, run]) for run in runs),
         )
@@ -157,7 +158,8 @@ def tile_attend_grls_pl_kernel(tc, Pc, xT, xE, er, offs, out_0, out_1, out_2):
 
         factor = keep.tile([P, SLOTS], F32, name="factor", tag="factor")
         summed = keep.tile([P, RUNS, P], F32, name="summed")
-        up0 = keep.tile([P, SLOTS], F32, name="up0")
+        up_early = keep.tile([P, 2, SLOTS], F32, name="up_early", tag="up_early")
+        up0 = up_early[:, 0, :]
         spreads = []
         k_er_early = []
         for b in range(2):
@@ -184,12 +186,10 @@ def tile_attend_grls_pl_kernel(tc, Pc, xT, xE, er, offs, out_0, out_1, out_2):
         for b in range(2):
             nc.vector.tensor_tensor(factor[:, runs[b]], spreads[b][:], er_listed[:, runs[b]], MULT)
         nc.vector.tensor_tensor(factor[:, halves[1]], late_flat, er_listed[:, halves[1]], MULT)
-
-        up1 = keep.tile([P, SLOTS], F32, name="up1", tag="up1")
-        nc.vector.tensor_tensor(up1[:, halves[0]], k1[:, halves[0]], factor[:, halves[0]], MULT)
-        nc.vector.tensor_tensor(up0[:, halves[1]], k0[:, halves[1]], factor[:, halves[1]], MULT)
-        nc.vector.tensor_tensor(up1[:, halves[1]], k1[:, halves[1]], factor[:, halves[1]], MULT)
-        up_late = keep.tile([P, 2, SLOTS], F32, name="up_late", tag="k_lane1")
+        nc.vector.tensor_tensor(up_early[:, 1, halves[0]], k1[:, halves[0]], factor[:, halves[0]], MULT)
+        both = factor[:, halves[1]].unsqueeze(1).to_broadcast([P, 2, HALF])
+        nc.vector.tensor_tensor(up_early[:, :, halves[1]], k_early[:, :, halves[1]], both, MULT)
+        up_late = keep.tile([P, 2, SLOTS], F32, name="up_late", tag="k_early")
         for slots in halves:
             both = factor[:, slots].unsqueeze(1).to_broadcast([P, 2, HALF])
             nc.gpsimd.tensor_tensor(up_late[:, :, slots], k_late[:, :, slots], both, MULT)
@@ -201,7 +201,7 @@ def tile_attend_grls_pl_kernel(tc, Pc, xT, xE, er, offs, out_0, out_1, out_2):
             nc.sync.dma_start(out_rows[:, t, :], windows[t][:])
 
         vector_pairs = keep.tile([P, UNITS - SCALAR_UNITS, 2, UNIT, 2], BF16, name="vector_pairs", tag="factor")
-        scalar_pairs = keep.tile([P, SCALAR_UNITS, 2, UNIT, 2], BF16, name="scalar_pairs", tag="up1")
+        scalar_pairs = keep.tile([P, SCALAR_UNITS, 2, UNIT, 2], BF16, name="scalar_pairs", tag="up_early")
 
         def pairs(first, last):
             if first < SCALAR_UNITS:
@@ -213,11 +213,11 @@ def tile_attend_grls_pl_kernel(tc, Pc, xT, xE, er, offs, out_0, out_1, out_2):
             target = pairs(first, last)[:, :, t // 2, :, t % 2].rearrange("p n (h c) -> p h n c", h=2)
             copy_on(nc, engine, target, source)
 
-        for slots in halves:
-            scatter_on_scalar(0, slots, up0[:, slots])
-        store_lane(0)
-        nc.vector.tensor_copy(out=listed(windows[1][:], every), in_=up1[:])
-        store_lane(1)
+        for t in range(2):
+            scatter_on_scalar(t, halves[0], up_early[:, t, halves[0]])
+        for t in range(2):
+            nc.vector.tensor_copy(out=listed(windows[t][:], halves[1]), in_=up_early[:, t, halves[1]])
+            store_lane(t)
         for slots in halves:
             for t in (2, 3):
                 scatter_on_scalar(t, slots, up_late[:, t - 2, slots])

@@ -259,10 +259,10 @@ def tile_attend_grls_pl_kernel(tc, Pc, xT, xE, er, offs, out_0, out_1, out_2):
         for first in (0, 2, 8, 10, 12, 14):
             merge("scalar", first, first + 2)
         merge("vector", 4, 8)
-        for first in range(0, UNITS, 4):
-            quantise(first, first + 2)
-            quantise(first + 2, first + 4)
-            store(first, first + 4)
+        for first, last in ((0, 6), (6, 12), (12, 16)):
+            for unit in range(first, last, 2):
+                quantise(unit, unit + 2)
+            store(first, last)
         scales_out = out_2[0].bitcast(I32).rearrange("r (j c) -> j r c", j=4)
         for quadrant in range(4):
             queue = nc.sync if quadrant % 2 == 0 else nc.scalar

@@ -190,9 +190,9 @@ def tile_attend_grls_pl_kernel(tc, Pc, xT, xE, er, offs, out_0, out_1, out_2):
         both = factor[:, halves[1]].unsqueeze(1).to_broadcast([P, 2, HALF])
         nc.vector.tensor_tensor(up_early[:, :, halves[1]], k_early[:, :, halves[1]], both, MULT)
         up_late = keep.tile([P, 2, SLOTS], F32, name="up_late", tag="k_early")
-        for slots in halves:
-            both = factor[:, slots].unsqueeze(1).to_broadcast([P, 2, HALF])
-            nc.gpsimd.tensor_tensor(up_late[:, :, slots], k_late[:, :, slots], both, MULT)
+        for v in range(2):
+            nc.gpsimd.tensor_tensor(up_late[:, v, halves[0]], k_late[:, v, halves[0]], factor[:, halves[0]], MULT)
+        nc.gpsimd.tensor_tensor(up_late[:, :, halves[1]], k_late[:, :, halves[1]], both, MULT)
 
         def scatter_on_scalar(t, slots, source):
             nc.scalar.activation(out=listed(windows[t][:], slots), in_=source, func=COPY)

@@ -61,7 +61,7 @@ def tile_attend_grls_pl_kernel(tc, Pc, xT, xE, er, offs, out_0, out_1, out_2):
             nc.sync.dma_start(xT_sb[u][:], xT_rows[:, 2 * u : 2 * u + 2, :])
         pc_sb = keep.tile([P, LANES, SLOTS], F32, name="pc_sb")
         nc.sync.dma_start(pc_sb[:], Pc.rearrange("(p j) e -> p j e", j=LANES))
-        xE_sb = [keep.tile([P, TABLE], F32, name=f"xE{t}") for t in range(LANES)]
+        xE_sb = [keep.tile([P, TABLE], F32, name=f"xE{t}", tag=f"xE{t}") for t in range(LANES)]
         for t in range(LANES):
             nc.sync.dma_start(xE_sb[t][:], xE_rows[:, t, :])
 
@@ -116,14 +116,13 @@ def tile_attend_grls_pl_kernel(tc, Pc, xT, xE, er, offs, out_0, out_1, out_2):
                 out=pc_codes[:, cols].bitcast(FP8X4), scales=pc_scales[:, cols], in_=pc_grouped[:, first:end].rearrange("p t m j -> p (t m j)")
             )
 
-        k_early = keep.tile([P, 2, SLOTS], F32, name="k_early", tag="k_early")
-        k0 = k_early[:, 0, :]
-        k1 = k_early[:, 1, :]
+        k0 = keep.tile([P, SLOTS], F32, name="k0")
+        k1 = [keep.tile([P, HALF], F32, name=f"k1{h}", tag=f"k1{h}") for h in range(2)]
         k_late = keep.tile([P, 2, SLOTS], F32, name="k_late")
         pieces = (
             (0, halves[0], "k0", k0[:, halves[0]]),
             (0, halves[1], "spare1", k0[:, halves[1]]),
-            (1, every, "k1", k1),
+            (1, every, "k1", None),
             (2, every, "k0", k_late[:, 0, :]),
             (3, every, "k1", k_late[:, 1, :]),
         )
@@ -138,14 +137,18 @@ def tile_attend_grls_pl_kernel(tc, Pc, xT, xE, er, offs, out_0, out_1, out_2):
                 start=True,
                 stop=True,
             )
-            nc.scalar.copy(out=target, in_=k_bank[:])
+            if t == 1:
+                for h in range(2):
+                    nc.scalar.copy(out=k1[h][:], in_=k_bank[:, halves[h]])
+            else:
+                nc.scalar.copy(out=target, in_=k_bank[:])
 
         sums = [psum.tile([P, P], F32, name=f"sums{b}", tag=f"sums{b}") for b in range(RUNS)]
         for b in range(RUNS):
             nc.tensor.matmul(sums[b][:], identity[:], identity[:], start=True, stop=False, is_transpose=True)
         cuts = (
             tuple((half, k0[:, half]) for half in halves),
-            ((every, k1),),
+            tuple((halves[h], k1[h][:]) for h in range(2)),
             ((every, k_late[:, 0, :]),),
             tuple((run, k_late[:, 1, run]) for run in runs),
         )
@@ -158,8 +161,10 @@ def tile_attend_grls_pl_kernel(tc, Pc, xT, xE, er, offs, out_0, out_1, out_2):
 
         factor = keep.tile([P, SLOTS], F32, name="factor", tag="factor")
         summed = keep.tile([P, RUNS, P], F32, name="summed")
-        up_early = keep.tile([P, 2, SLOTS], F32, name="up_early", tag="up_early")
-        up0 = up_early[:, 0, :]
+        up_early = keep.tile([P, 3, HALF], F32, name="up_early", tag="up_early")
+        up0 = up_early[:, :2, :].rearrange("p h c -> p (h c)")
+        k_er_late = keep.tile([P, HALF], F32, name="k_er_late", tag="xE3")
+        nc.gpsimd.tensor_tensor(k_er_late[:], k0[:, halves[1]], er_listed[:, halves[1]], MULT)
         spreads = []
         k_er_early = []
         for b in range(2):
@@ -186,12 +191,14 @@ def tile_attend_grls_pl_kernel(tc, Pc, xT, xE, er, offs, out_0, out_1, out_2):
         for b in range(2):
             nc.vector.tensor_tensor(factor[:, runs[b]], spreads[b][:], er_listed[:, runs[b]], MULT)
         nc.vector.tensor_tensor(factor[:, halves[1]], late_flat, er_listed[:, halves[1]], MULT)
-        nc.vector.tensor_tensor(up_early[:, 1, halves[0]], k1[:, halves[0]], factor[:, halves[0]], MULT)
-        both = factor[:, halves[1]].unsqueeze(1).to_broadcast([P, 2, HALF])
-        nc.vector.tensor_tensor(up_early[:, :, halves[1]], k_early[:, :, halves[1]], both, MULT)
-        up_late = keep.tile([P, 2, SLOTS], F32, name="up_late", tag="k_early")
+        nc.vector.tensor_tensor(up0[:, halves[1]], late_flat, k_er_late[:], MULT)
+        nc.vector.tensor_tensor(up_early[:, 2, :], k1[0][:], factor[:, halves[0]], MULT)
+        up1_late = keep.tile([P, HALF], F32, name="up1_late", tag="k10")
+        nc.gpsimd.tensor_tensor(up1_late[:], k1[1][:], factor[:, halves[1]], MULT)
+        up_late = keep.tile([P, 2, SLOTS], F32, name="up_late", tag="k11")
         for v in range(2):
             nc.gpsimd.tensor_tensor(up_late[:, v, halves[0]], k_late[:, v, halves[0]], factor[:, halves[0]], MULT)
+        both = factor[:, halves[1]].unsqueeze(1).to_broadcast([P, 2, HALF])
         nc.gpsimd.tensor_tensor(up_late[:, :, halves[1]], k_late[:, :, halves[1]], both, MULT)
 
         def scatter_on_scalar(t, slots, source):
@@ -214,9 +221,9 @@ def tile_attend_grls_pl_kernel(tc, Pc, xT, xE, er, offs, out_0, out_1, out_2):
             copy_on(nc, engine, target, source)
 
         for t in range(2):
-            scatter_on_scalar(t, halves[0], up_early[:, t, halves[0]])
-        for t in range(2):
-            nc.vector.tensor_copy(out=listed(windows[t][:], halves[1]), in_=up_early[:, t, halves[1]])
+            scatter_on_scalar(t, halves[0], up_early[:, 2 * t, :])
+        for t, product in enumerate((up_early[:, 1, :], up1_late[:])):
+            nc.vector.tensor_copy(out=listed(windows[t][:], halves[1]), in_=product)
             store_lane(t)
         for slots in halves:
             for t in (2, 3):

@@ -24,7 +24,7 @@ FLOPS = 2 * 512 * 512 * 512
 SCALAR_DEAL = 72
 UNIT = 128
 UNITS = TABLE // UNIT
-SCALAR_UNITS = 2
+SCALAR_UNITS = 3
 PLANE = TABLE // 4
 
 
@@ -161,10 +161,12 @@ def tile_attend_grls_pl_kernel(tc, Pc, xT, xE, er, offs, out_0, out_1, out_2):
 
         factor = keep.tile([P, SLOTS], F32, name="factor", tag="factor")
         summed = keep.tile([P, RUNS, P], F32, name="summed")
-        up_early = keep.tile([P, 3, HALF], F32, name="up_early", tag="up_early")
-        up0 = up_early[:, :2, :].rearrange("p h c -> p (h c)")
-        k_er_late = keep.tile([P, HALF], F32, name="k_er_late", tag="xE3")
-        nc.gpsimd.tensor_tensor(k_er_late[:], k0[:, halves[1]], er_listed[:, halves[1]], MULT)
+        zeros = keep.tile([P, P], F32, name="zeros", tag="zeros")
+        nc.gpsimd.memset(zeros[:], 0.0)
+        up0 = keep.tile([P, SLOTS], F32, name="up0", tag="up0")
+        k_er_late = keep.tile([P, HALF + P], F32, name="k_er_late", tag="xE3")
+        nc.gpsimd.tensor_tensor(k_er_late[:, HALF:], k_late[:, 0, runs[0]], er_listed[:, runs[0]], MULT)
+        nc.gpsimd.tensor_tensor(k_er_late[:, :HALF], k0[:, halves[1]], er_listed[:, halves[1]], MULT)
         spreads = []
         k_er_early = []
         for b in range(2):
@@ -177,8 +179,10 @@ def tile_attend_grls_pl_kernel(tc, Pc, xT, xE, er, offs, out_0, out_1, out_2):
             spreads.append(spread)
             k_er_early.append(keep.tile([P, P], F32, name=f"k_er_early{b}", tag=f"early{b}"))
             nc.vector.tensor_tensor(k_er_early[b][:], k0[:, runs[b]], er_listed[:, runs[b]], MULT)
-        for b in range(2):
-            nc.vector.tensor_tensor(up0[:, runs[b]], spreads[b][:], k_er_early[b][:], MULT)
+        up2_first = keep.tile([P, P], F32, name="up2_first")
+        nc.vector.tensor_tensor(up0[:, runs[0]], spreads[0][:], k_er_early[0][:], MULT)
+        nc.vector.tensor_tensor(up2_first[:], spreads[0][:], k_er_late[:, HALF:], MULT)
+        nc.vector.tensor_tensor(up0[:, runs[1]], spreads[1][:], k_er_early[1][:], MULT)
         late_denominator = keep.tile([P, 2], F32, name="late_denominator")
         for i in range(2):
             nc.scalar.activation(out=summed[:, 2 + i, :], in_=sums[2 + i][:], func=COPY, accum_out=late_denominator[:, i : i + 1])
@@ -190,16 +194,18 @@ def tile_attend_grls_pl_kernel(tc, Pc, xT, xE, er, offs, out_0, out_1, out_2):
         late_flat = late_spread[:].rearrange("p i m -> p (i m)")
         for b in range(2):
             nc.vector.tensor_tensor(factor[:, runs[b]], spreads[b][:], er_listed[:, runs[b]], MULT)
+        up1_early = keep.tile([P, HALF], F32, name="up1_early")
+        nc.gpsimd.tensor_tensor(up1_early[:], k1[0][:], factor[:, halves[0]], MULT)
         nc.vector.tensor_tensor(factor[:, halves[1]], late_flat, er_listed[:, halves[1]], MULT)
-        nc.vector.tensor_tensor(up0[:, halves[1]], late_flat, k_er_late[:], MULT)
-        nc.vector.tensor_tensor(up_early[:, 2, :], k1[0][:], factor[:, halves[0]], MULT)
-        up1_late = keep.tile([P, HALF], F32, name="up1_late", tag="k10")
+        nc.vector.tensor_tensor(up0[:, halves[1]], late_flat, k_er_late[:, :HALF], MULT)
+        nc.vector.tensor_tensor(listed(windows[2][:], runs[0]), up2_first[:], zeros[:], mybir.AluOpType.add)
+        rest = slice(P, SLOTS)
+        up_late = keep.tile([P, 2, SLOTS], F32, name="up_late", tag="xE3")
+        nc.gpsimd.tensor_tensor(up_late[:, 1, halves[0]], k_late[:, 1, halves[0]], factor[:, halves[0]], MULT)
+        up1_late = keep.tile([P, HALF], F32, name="up1_late", tag="zeros")
         nc.gpsimd.tensor_tensor(up1_late[:], k1[1][:], factor[:, halves[1]], MULT)
-        up_late = keep.tile([P, 2, SLOTS], F32, name="up_late", tag="k11")
-        for v in range(2):
-            nc.gpsimd.tensor_tensor(up_late[:, v, halves[0]], k_late[:, v, halves[0]], factor[:, halves[0]], MULT)
-        both = factor[:, halves[1]].unsqueeze(1).to_broadcast([P, 2, HALF])
-        nc.gpsimd.tensor_tensor(up_late[:, :, halves[1]], k_late[:, :, halves[1]], both, MULT)
+        nc.gpsimd.tensor_tensor(up_late[:, 0, rest], k_late[:, 0, rest], factor[:, rest], MULT)
+        nc.gpsimd.tensor_tensor(up_late[:, 1, halves[1]], k_late[:, 1, halves[1]], factor[:, halves[1]], MULT)
 
         def scatter_on_scalar(t, slots, source):
             nc.scalar.activation(out=listed(windows[t][:], slots), in_=source, func=COPY)
@@ -208,7 +214,7 @@ def tile_attend_grls_pl_kernel(tc, Pc, xT, xE, er, offs, out_0, out_1, out_2):
             nc.sync.dma_start(out_rows[:, t, :], windows[t][:])
 
         vector_pairs = keep.tile([P, UNITS - SCALAR_UNITS, 2, UNIT, 2], BF16, name="vector_pairs", tag="factor")
-        scalar_pairs = keep.tile([P, SCALAR_UNITS, 2, UNIT, 2], BF16, name="scalar_pairs", tag="up_early")
+        scalar_pairs = keep.tile([P, SCALAR_UNITS, 2, UNIT, 2], BF16, name="scalar_pairs", tag="zeros")
 
         def pairs(first, last):
             if first < SCALAR_UNITS:
@@ -220,14 +226,14 @@ def tile_attend_grls_pl_kernel(tc, Pc, xT, xE, er, offs, out_0, out_1, out_2):
             target = pairs(first, last)[:, :, t // 2, :, t % 2].rearrange("p n (h c) -> p h n c", h=2)
             copy_on(nc, engine, target, source)
 
-        for t in range(2):
-            scatter_on_scalar(t, halves[0], up_early[:, 2 * t, :])
-        for t, product in enumerate((up_early[:, 1, :], up1_late[:])):
+        scatter_on_scalar(0, halves[0], up0[:, halves[0]])
+        scatter_on_scalar(1, halves[0], up1_early[:])
+        for t, product in enumerate((up0[:, halves[1]], up1_late[:])):
             nc.vector.tensor_copy(out=listed(windows[t][:], halves[1]), in_=product)
             store_lane(t)
-        for slots in halves:
-            for t in (2, 3):
-                scatter_on_scalar(t, slots, up_late[:, t - 2, slots])
+        scatter_on_scalar(3, halves[0], up_late[:, 1, halves[0]])
+        scatter_on_scalar(2, rest, up_late[:, 0, rest])
+        scatter_on_scalar(3, halves[1], up_late[:, 1, halves[1]])
         for t in (2, 3):
             store_lane(t)
         for t in range(3):
@@ -261,11 +267,11 @@ def tile_attend_grls_pl_kernel(tc, Pc, xT, xE, er, offs, out_0, out_1, out_2):
             cols = slice(first * UNIT, last * UNIT)
             nc.sync.dma_start(words_out[:, cols], codes[:, cols].bitcast(I32))
 
-        for first, last in ((2, 4), (4, 10), (10, 16)):
+        for first, last in ((3, 5), (5, 10), (10, 16)):
             write_lane("vector", 3, first, last)
-        for first in (0, 2, 8, 10, 12, 14):
-            merge("scalar", first, first + 2)
-        merge("vector", 4, 8)
+        for first, last in ((0, 3), (3, 5), (8, 10), (10, 12), (12, 14), (14, 16)):
+            merge("scalar", first, last)
+        merge("vector", 5, 8)
         for first, last in ((0, 6), (6, 12), (12, 16)):
             for unit in range(first, last, 2):
                 quantise(unit, unit + 2)

@@ -61,7 +61,7 @@ def tile_attend_grls_pl_kernel(tc, Pc, xT, xE, er, offs, out_0, out_1, out_2):
             nc.sync.dma_start(xT_sb[u][:], xT_rows[:, 2 * u : 2 * u + 2, :])
         pc_sb = keep.tile([P, LANES, SLOTS], F32, name="pc_sb")
         nc.sync.dma_start(pc_sb[:], Pc.rearrange("(p j) e -> p j e", j=LANES))
-        xE_sb = [keep.tile([P, TABLE], F32, name=f"xE{t}", tag=f"xE{t}") for t in range(LANES)]
+        xE_sb = [keep.tile([P, TABLE], F32, name=f"xE{t}") for t in range(LANES)]
         for t in range(LANES):
             nc.sync.dma_start(xE_sb[t][:], xE_rows[:, t, :])
 
@@ -116,12 +116,12 @@ def tile_attend_grls_pl_kernel(tc, Pc, xT, xE, er, offs, out_0, out_1, out_2):
                 out=pc_codes[:, cols].bitcast(FP8X4), scales=pc_scales[:, cols], in_=pc_grouped[:, first:end].rearrange("p t m j -> p (t m j)")
             )
 
-        k0 = keep.tile([P, SLOTS], F32, name="k0")
+        k0 = [keep.tile([P, HALF], F32, name=f"k0{h}", tag=f"k0{h}") for h in range(2)]
         k1 = [keep.tile([P, HALF], F32, name=f"k1{h}", tag=f"k1{h}") for h in range(2)]
         k_late = keep.tile([P, 2, SLOTS], F32, name="k_late")
         pieces = (
-            (0, halves[0], "k0", k0[:, halves[0]]),
-            (0, halves[1], "spare1", k0[:, halves[1]]),
+            (0, halves[0], "k0", k0[0][:]),
+            (0, halves[1], "spare1", k0[1][:]),
             (1, every, "k1", None),
             (2, every, "k0", k_late[:, 0, :]),
             (3, every, "k1", k_late[:, 1, :]),
@@ -147,7 +147,7 @@ def tile_attend_grls_pl_kernel(tc, Pc, xT, xE, er, offs, out_0, out_1, out_2):
         for b in range(RUNS):
             nc.tensor.matmul(sums[b][:], identity[:], identity[:], start=True, stop=False, is_transpose=True)
         cuts = (
-            tuple((half, k0[:, half]) for half in halves),
+            tuple((halves[h], k0[h][:]) for h in range(2)),
             tuple((halves[h], k1[h][:]) for h in range(2)),
             ((every, k_late[:, 0, :]),),
             tuple((run, k_late[:, 1, run]) for run in runs),
@@ -164,9 +164,6 @@ def tile_attend_grls_pl_kernel(tc, Pc, xT, xE, er, offs, out_0, out_1, out_2):
         zeros = keep.tile([P, P], F32, name="zeros", tag="zeros")
         nc.gpsimd.memset(zeros[:], 0.0)
         up0 = keep.tile([P, SLOTS], F32, name="up0", tag="up0")
-        k_er_late = keep.tile([P, HALF + P], F32, name="k_er_late", tag="xE3")
-        nc.gpsimd.tensor_tensor(k_er_late[:, HALF:], k_late[:, 0, runs[0]], er_listed[:, runs[0]], MULT)
-        nc.gpsimd.tensor_tensor(k_er_late[:, :HALF], k0[:, halves[1]], er_listed[:, halves[1]], MULT)
         spreads = []
         k_er_early = []
         for b in range(2):
@@ -178,7 +175,10 @@ def tile_attend_grls_pl_kernel(tc, Pc, xT, xE, er, offs, out_0, out_1, out_2):
             nc.tensor.transpose(spread[:], inverse[:].to_broadcast([P, P]), identity[:])
             spreads.append(spread)
             k_er_early.append(keep.tile([P, P], F32, name=f"k_er_early{b}", tag=f"early{b}"))
-            nc.vector.tensor_tensor(k_er_early[b][:], k0[:, runs[b]], er_listed[:, runs[b]], MULT)
+            nc.vector.tensor_tensor(k_er_early[b][:], k0[0][:, runs[b]], er_listed[:, runs[b]], MULT)
+        k_er_late = keep.tile([P, HALF + P], F32, name="k_er_late", tag="k00")
+        nc.gpsimd.tensor_tensor(k_er_late[:, HALF:], k_late[:, 0, runs[0]], er_listed[:, runs[0]], MULT)
+        nc.gpsimd.tensor_tensor(k_er_late[:, :HALF], k0[1][:], er_listed[:, halves[1]], MULT)
         up2_first = keep.tile([P, P], F32, name="up2_first")
         nc.vector.tensor_tensor(up0[:, runs[0]], spreads[0][:], k_er_early[0][:], MULT)
         nc.vector.tensor_tensor(up2_first[:], spreads[0][:], k_er_late[:, HALF:], MULT)
@@ -200,7 +200,7 @@ def tile_attend_grls_pl_kernel(tc, Pc, xT, xE, er, offs, out_0, out_1, out_2):
         nc.vector.tensor_tensor(up0[:, halves[1]], late_flat, k_er_late[:, :HALF], MULT)
         nc.vector.tensor_tensor(listed(windows[2][:], runs[0]), up2_first[:], zeros[:], mybir.AluOpType.add)
         rest = slice(P, SLOTS)
-        up_late = keep.tile([P, 2, SLOTS], F32, name="up_late", tag="xE3")
+        up_late = keep.tile([P, 2, SLOTS], F32, name="up_late", tag="k00")
         nc.gpsimd.tensor_tensor(up_late[:, 1, halves[0]], k_late[:, 1, halves[0]], factor[:, halves[0]], MULT)
         up1_late = keep.tile([P, HALF], F32, name="up1_late", tag="zeros")
         nc.gpsimd.tensor_tensor(up1_late[:], k1[1][:], factor[:, halves[1]], MULT)

@@ -174,15 +174,15 @@ def tile_attend_grls_pl_kernel(tc, Pc, xT, xE, er, offs, out_0, out_1, out_2):
             spread = psum.tile([P, P], F32, name=f"spread{b}", tag=f"k{b}")
             nc.tensor.transpose(spread[:], inverse[:].to_broadcast([P, P]), identity[:])
             spreads.append(spread)
-            k_er_early.append(keep.tile([P, P], F32, name=f"k_er_early{b}", tag=f"early{b}"))
-            nc.vector.tensor_tensor(k_er_early[b][:], k0[0][:, runs[b]], er_listed[:, runs[b]], MULT)
-        k_er_late = keep.tile([P, HALF + P], F32, name="k_er_late", tag="k00")
-        nc.gpsimd.tensor_tensor(k_er_late[:, HALF:], k_late[:, 0, runs[0]], er_listed[:, runs[0]], MULT)
-        nc.gpsimd.tensor_tensor(k_er_late[:, :HALF], k0[1][:], er_listed[:, halves[1]], MULT)
+            k_er_early.append(keep.tile([P, 2 - b, P], F32, name=f"k_er_early{b}", tag=f"early{b}"))
+            nc.vector.tensor_tensor(k_er_early[b][:, 0, :], k0[0][:, runs[b]], er_listed[:, runs[b]], MULT)
+        k2_er = k_er_early[0][:, 1, :]
+        nc.vector.tensor_tensor(k2_er, k_late[:, 0, runs[0]], er_listed[:, runs[0]], MULT)
+        k_er_late = keep.tile([P, HALF], F32, name="k_er_late", tag="k00")
+        nc.gpsimd.tensor_tensor(k_er_late[:], k0[1][:], er_listed[:, halves[1]], MULT)
         up2_first = keep.tile([P, P], F32, name="up2_first")
-        nc.vector.tensor_tensor(up0[:, runs[0]], spreads[0][:], k_er_early[0][:], MULT)
-        nc.vector.tensor_tensor(up2_first[:], spreads[0][:], k_er_late[:, HALF:], MULT)
-        nc.vector.tensor_tensor(up0[:, runs[1]], spreads[1][:], k_er_early[1][:], MULT)
+        nc.vector.tensor_tensor(up0[:, runs[0]], spreads[0][:], k_er_early[0][:, 0, :], MULT)
+        nc.vector.tensor_tensor(up0[:, runs[1]], spreads[1][:], k_er_early[1][:, 0, :], MULT)
         late_denominator = keep.tile([P, 2], F32, name="late_denominator")
         for i in range(2):
             nc.scalar.activation(out=summed[:, 2 + i, :], in_=sums[2 + i][:], func=COPY, accum_out=late_denominator[:, i : i + 1])
@@ -194,10 +194,11 @@ def tile_attend_grls_pl_kernel(tc, Pc, xT, xE, er, offs, out_0, out_1, out_2):
         late_flat = late_spread[:].rearrange("p i m -> p (i m)")
         for b in range(2):
             nc.vector.tensor_tensor(factor[:, runs[b]], spreads[b][:], er_listed[:, runs[b]], MULT)
+        nc.vector.tensor_tensor(up2_first[:], spreads[0][:], k2_er, MULT)
         up1_early = keep.tile([P, HALF], F32, name="up1_early")
         nc.gpsimd.tensor_tensor(up1_early[:], k1[0][:], factor[:, halves[0]], MULT)
         nc.vector.tensor_tensor(factor[:, halves[1]], late_flat, er_listed[:, halves[1]], MULT)
-        nc.vector.tensor_tensor(up0[:, halves[1]], late_flat, k_er_late[:, :HALF], MULT)
+        nc.vector.tensor_tensor(up0[:, halves[1]], late_flat, k_er_late[:], MULT)
         nc.vector.tensor_tensor(listed(windows[2][:], runs[0]), up2_first[:], zeros[:], mybir.AluOpType.add)
         rest = slice(P, SLOTS)
         up_late = keep.tile([P, 2, SLOTS], F32, name="up_late", tag="k00")

@@ -118,13 +118,14 @@ def tile_attend_grls_pl_kernel(tc, Pc, xT, xE, er, offs, out_0, out_1, out_2):
 
         k0 = [keep.tile([P, HALF], F32, name=f"k0{h}", tag=f"k0{h}") for h in range(2)]
         k1 = [keep.tile([P, HALF], F32, name=f"k1{h}", tag=f"k1{h}") for h in range(2)]
-        k_late = keep.tile([P, 2, SLOTS], F32, name="k_late")
+        k2 = keep.tile([P, SLOTS], F32, name="k2", tag="k2")
+        k3 = keep.tile([P, SLOTS], F32, name="k3")
         pieces = (
             (0, halves[0], "k0", k0[0][:]),
             (0, halves[1], "spare1", k0[1][:]),
             (1, every, "k1", None),
-            (2, every, "k0", k_late[:, 0, :]),
-            (3, every, "k1", k_late[:, 1, :]),
+            (2, every, "k0", k2[:]),
+            (3, every, "k1", k3[:]),
         )
         for n, (t, slots, tag, target) in enumerate(pieces):
             k_bank = psum.tile([P, slots.stop - slots.start], F32, name=f"k_bank{n}", tag=tag)
@@ -149,8 +150,8 @@ def tile_attend_grls_pl_kernel(tc, Pc, xT, xE, er, offs, out_0, out_1, out_2):
         cuts = (
             tuple((halves[h], k0[h][:]) for h in range(2)),
             tuple((halves[h], k1[h][:]) for h in range(2)),
-            ((every, k_late[:, 0, :]),),
-            tuple((run, k_late[:, 1, run]) for run in runs),
+            ((every, k2[:]),),
+            tuple((run, k3[:, run]) for run in runs),
         )
         for t in range(LANES):
             q = keep.tile([P, SLOTS], F32, name=f"q{t}")
@@ -177,7 +178,7 @@ def tile_attend_grls_pl_kernel(tc, Pc, xT, xE, er, offs, out_0, out_1, out_2):
             k_er_early.append(keep.tile([P, 2 - b, P], F32, name=f"k_er_early{b}", tag=f"early{b}"))
             nc.vector.tensor_tensor(k_er_early[b][:, 0, :], k0[0][:, runs[b]], er_listed[:, runs[b]], MULT)
         k2_er = k_er_early[0][:, 1, :]
-        nc.vector.tensor_tensor(k2_er, k_late[:, 0, runs[0]], er_listed[:, runs[0]], MULT)
+        nc.vector.tensor_tensor(k2_er, k2[:, runs[0]], er_listed[:, runs[0]], MULT)
         k_er_late = keep.tile([P, HALF], F32, name="k_er_late", tag="k00")
         nc.gpsimd.tensor_tensor(k_er_late[:], k0[1][:], er_listed[:, halves[1]], MULT)
         up2_first = keep.tile([P, P], F32, name="up2_first")
@@ -202,11 +203,11 @@ def tile_attend_grls_pl_kernel(tc, Pc, xT, xE, er, offs, out_0, out_1, out_2):
         nc.vector.tensor_tensor(listed(windows[2][:], runs[0]), up2_first[:], zeros[:], mybir.AluOpType.add)
         rest = slice(P, SLOTS)
         up_late = keep.tile([P, 2, SLOTS], F32, name="up_late", tag="k00")
-        nc.gpsimd.tensor_tensor(up_late[:, 1, halves[0]], k_late[:, 1, halves[0]], factor[:, halves[0]], MULT)
+        nc.gpsimd.tensor_tensor(up_late[:, 1, halves[0]], k3[:, halves[0]], factor[:, halves[0]], MULT)
         up1_late = keep.tile([P, HALF], F32, name="up1_late", tag="zeros")
         nc.gpsimd.tensor_tensor(up1_late[:], k1[1][:], factor[:, halves[1]], MULT)
-        nc.gpsimd.tensor_tensor(up_late[:, 0, rest], k_late[:, 0, rest], factor[:, rest], MULT)
-        nc.gpsimd.tensor_tensor(up_late[:, 1, halves[1]], k_late[:, 1, halves[1]], factor[:, halves[1]], MULT)
+        nc.gpsimd.tensor_tensor(up_late[:, 0, rest], k2[:, rest], factor[:, rest], MULT)
+        nc.gpsimd.tensor_tensor(up_late[:, 1, halves[1]], k3[:, halves[1]], factor[:, halves[1]], MULT)
 
         def scatter_on_scalar(t, slots, source):
             nc.scalar.activation(out=listed(windows[t][:], slots), in_=source, func=COPY)
@@ -214,7 +215,7 @@ def tile_attend_grls_pl_kernel(tc, Pc, xT, xE, er, offs, out_0, out_1, out_2):
         def store_lane(t):
             nc.sync.dma_start(out_rows[:, t, :], windows[t][:])
 
-        vector_pairs = keep.tile([P, UNITS - SCALAR_UNITS, 2, UNIT, 2], BF16, name="vector_pairs", tag="factor")
+        vector_pairs = keep.tile([P, UNITS - SCALAR_UNITS, 2, UNIT, 2], BF16, name="vector_pairs", tag="k2")
         scalar_pairs = keep.tile([P, SCALAR_UNITS, 2, UNIT, 2], BF16, name="scalar_pairs", tag="zeros")
 
         def pairs(first, last):

@@ -22,6 +22,7 @@ RUNS = SLOTS // P
 FLOPS = 2 * 512 * 512 * 512
 
 SCALAR_DEAL = 72
+ADDED = 160
 UNIT = 128
 UNITS = TABLE // UNIT
 SCALAR_UNITS = 3
@@ -162,7 +163,7 @@ def tile_attend_grls_pl_kernel(tc, Pc, xT, xE, er, offs, out_0, out_1, out_2):
 
         factor = keep.tile([P, SLOTS], F32, name="factor", tag="factor")
         summed = keep.tile([P, RUNS, P], F32, name="summed")
-        zeros = keep.tile([P, P], F32, name="zeros", tag="zeros")
+        zeros = keep.tile([P, ADDED], F32, name="zeros", tag="zeros")
         nc.gpsimd.memset(zeros[:], 0.0)
         up0 = keep.tile([P, SLOTS], F32, name="up0", tag="up0")
         spreads = []
@@ -175,15 +176,15 @@ def tile_attend_grls_pl_kernel(tc, Pc, xT, xE, er, offs, out_0, out_1, out_2):
             spread = psum.tile([P, P], F32, name=f"spread{b}", tag=f"k{b}")
             nc.tensor.transpose(spread[:], inverse[:].to_broadcast([P, P]), identity[:])
             spreads.append(spread)
-            k_er_early.append(keep.tile([P, 2 - b, P], F32, name=f"k_er_early{b}", tag=f"early{b}"))
-            nc.vector.tensor_tensor(k_er_early[b][:, 0, :], k0[0][:, runs[b]], er_listed[:, runs[b]], MULT)
-        k2_er = k_er_early[0][:, 1, :]
-        nc.vector.tensor_tensor(k2_er, k2[:, runs[0]], er_listed[:, runs[0]], MULT)
+            k_er_early.append(keep.tile([P, P + (1 - b) * ADDED], F32, name=f"k_er_early{b}", tag=f"early{b}"))
+            nc.vector.tensor_tensor(k_er_early[b][:, :P], k0[0][:, runs[b]], er_listed[:, runs[b]], MULT)
+        k2_er = k_er_early[0][:, P:]
+        nc.vector.tensor_tensor(k2_er, k2[:, :ADDED], er_listed[:, :ADDED], MULT)
         k_er_late = keep.tile([P, HALF], F32, name="k_er_late", tag="k00")
         nc.gpsimd.tensor_tensor(k_er_late[:], k0[1][:], er_listed[:, halves[1]], MULT)
-        up2_first = keep.tile([P, P], F32, name="up2_first")
-        nc.vector.tensor_tensor(up0[:, runs[0]], spreads[0][:], k_er_early[0][:, 0, :], MULT)
-        nc.vector.tensor_tensor(up0[:, runs[1]], spreads[1][:], k_er_early[1][:, 0, :], MULT)
+        up2_first = keep.tile([P, ADDED], F32, name="up2_first")
+        nc.vector.tensor_tensor(up0[:, runs[0]], spreads[0][:], k_er_early[0][:, :P], MULT)
+        nc.vector.tensor_tensor(up0[:, runs[1]], spreads[1][:], k_er_early[1][:, :P], MULT)
         late_denominator = keep.tile([P, 2], F32, name="late_denominator")
         for i in range(2):
             nc.scalar.activation(out=summed[:, 2 + i, :], in_=sums[2 + i][:], func=COPY, accum_out=late_denominator[:, i : i + 1])
@@ -195,13 +196,14 @@ def tile_attend_grls_pl_kernel(tc, Pc, xT, xE, er, offs, out_0, out_1, out_2):
         late_flat = late_spread[:].rearrange("p i m -> p (i m)")
         for b in range(2):
             nc.vector.tensor_tensor(factor[:, runs[b]], spreads[b][:], er_listed[:, runs[b]], MULT)
-        nc.vector.tensor_tensor(up2_first[:], spreads[0][:], k2_er, MULT)
+        nc.vector.tensor_tensor(up2_first[:, :P], spreads[0][:], k2_er[:, :P], MULT)
+        nc.vector.tensor_tensor(up2_first[:, P:], spreads[1][:, : ADDED - P], k2_er[:, P:], MULT)
         up1_early = keep.tile([P, HALF], F32, name="up1_early")
         nc.gpsimd.tensor_tensor(up1_early[:], k1[0][:], factor[:, halves[0]], MULT)
         nc.vector.tensor_tensor(factor[:, halves[1]], late_flat, er_listed[:, halves[1]], MULT)
         nc.vector.tensor_tensor(up0[:, halves[1]], late_flat, k_er_late[:], MULT)
-        nc.vector.tensor_tensor(listed(windows[2][:], runs[0]), up2_first[:], zeros[:], mybir.AluOpType.add)
-        rest = slice(P, SLOTS)
+        nc.vector.tensor_tensor(listed(windows[2][:], slice(0, ADDED)), up2_first[:], zeros[:], mybir.AluOpType.add)
+        rest = slice(ADDED, SLOTS)
         up_late = keep.tile([P, 2, SLOTS], F32, name="up_late", tag="k00")
         nc.gpsimd.tensor_tensor(up_late[:, 1, halves[0]], k3[:, halves[0]], factor[:, halves[0]], MULT)
         up1_late = keep.tile([P, HALF], F32, name="up1_late", tag="zeros")
@@ -269,7 +271,7 @@ def tile_attend_grls_pl_kernel(tc, Pc, xT, xE, er, offs, out_0, out_1, out_2):
             cols = slice(first * UNIT, last * UNIT)
             nc.sync.dma_start(words_out[:, cols], codes[:, cols].bitcast(I32))
 
-        for first, last in ((3, 5), (5, 10), (10, 16)):
+        for first, last in ((3, 8), (8, 16)):
             write_lane("vector", 3, first, last)
         for first, last in ((0, 3), (3, 5), (8, 10), (10, 12), (12, 14), (14, 16)):
             merge("scalar", first, last)

from contextlib import ExitStack

import concourse.mybir as mybir
from concourse.masks import make_identity

F32 = mybir.dt.float32
BF16 = mybir.dt.bfloat16
I32 = mybir.dt.int32
U32 = mybir.dt.uint32
U16 = mybir.dt.uint16
U8 = mybir.dt.uint8
FP8X4 = mybir.dt.float8_e4m3fn_x4
MULT = mybir.AluOpType.mult
COPY = mybir.ActivationFunctionType.Copy

P = 128
LANES = 4
SLOTS = 512
TABLE = 2048
HALF = SLOTS // 2
RUNS = SLOTS // P
FLOPS = 2 * 512 * 512 * 512

SCALAR_DEAL = 72
ADDED = 160
UNIT = 128
UNITS = TABLE // UNIT
SCALAR_UNITS = 3
PLANE = TABLE // 4


def copy_on(nc, engine, out, in_):
    if engine == "scalar":
        nc.scalar.copy(out=out, in_=in_)
    else:
        nc.vector.tensor_copy(out=out, in_=in_)


def tile_attend_grls_pl_kernel(tc, Pc, xT, xE, er, offs, out_0, out_1, out_2):
    nc = tc.nc
    with ExitStack() as ctx:
        keep = ctx.enter_context(tc.tile_pool(name="keep", bufs=1))
        psum = ctx.enter_context(tc.psum_pool(name="psum", bufs=1))

        offsets = keep.tile([P, SLOTS // 16], U16, name="offsets")
        nc.sync.dma_start(offsets[:], offs)
        halves = [slice(h * HALF, (h + 1) * HALF) for h in range(2)]
        runs = [slice(b * P, (b + 1) * P) for b in range(RUNS)]

        def listed(window, slots):
            return window.indirect(offsets[:, slots.start // 16 : slots.stop // 16])

        every = slice(0, SLOTS)
        xT_rows = xT.rearrange("(p t) c -> p t c", t=LANES)
        xE_rows = xE.rearrange("(p t) c -> p t c", t=LANES)
        out_rows = out_0.rearrange("(p t) c -> p t c", t=LANES)

        er_upright = keep.tile([P, TABLE // P], F32, name="er_upright")
        nc.sync.dma_start(er_upright[:], er[0].rearrange("(p j) -> p j", p=P))
        xT_sb = [keep.tile([P, 2, TABLE], F32, name=f"xT{u}") for u in range(2)]
        for u in range(2):
            nc.sync.dma_start(xT_sb[u][:], xT_rows[:, 2 * u : 2 * u + 2, :])
        pc_sb = keep.tile([P, LANES, SLOTS], F32, name="pc_sb")
        nc.sync.dma_start(pc_sb[:], Pc.rearrange("(p j) e -> p j e", j=LANES))
        xE_sb = [keep.tile([P, TABLE], F32, name=f"xE{t}") for t in range(LANES)]
        for t in range(LANES):
            nc.sync.dma_start(xE_sb[t][:], xE_rows[:, t, :])

        windows = [keep.tile([P, TABLE], F32, name=f"window{t}") for t in range(LANES)]
        identity = keep.tile([P, P], F32, name="identity")
        for t in range(2):
            nc.vector.memset(windows[t][:], 0.0)
        make_identity(nc, identity[:])
        for t in range(2, LANES):
            nc.gpsimd.memset(windows[t][:], 0.0)

        er_sb = keep.tile([P, TABLE], F32, name="er_sb", tag="er_sb", align_bytes=64)
        er_places = er_sb[:].rearrange("p (m j) -> p m j", m=P)
        for n, tag in enumerate(("k0", "k1", "spare0", "spare1")):
            er_wide = psum.tile([P, 4, P], F32, name=f"er_wide{n}", tag=tag)
            for b in range(4):
                column = 4 * n + b
                nc.tensor.transpose(er_wide[:, b, :], er_upright[:, column : column + 1].to_broadcast([P, P]), identity[:])
            nc.scalar.activation(out=er_places[:, :, 4 * n : 4 * (n + 1)], in_=er_wide[:].rearrange("p b m -> p m b"), func=COPY)

        x_early = keep.tile([P, 2, SLOTS], F32, name="x_early", tag="x_early", align_bytes=64)
        for v in range(2):
            nc.vector.tensor_copy(out=x_early[:, v, :], in_=listed(xT_sb[0][:, v, :], every))
        er_listed = keep.tile([P, SLOTS], F32, name="er_listed")
        nc.vector.tensor_copy(out=er_listed[:], in_=listed(er_sb[:], every))
        x_grouped = keep.tile([P, SLOTS, LANES], BF16, name="x_grouped", tag="er_sb", align_bytes=64)
        x_codes = keep.tile([P, SLOTS], U32, name="x_codes", align_bytes=64)
        x_scales = keep.tile([P, SLOTS], U8, name="x_scales", align_bytes=64)
        nc.scalar.copy(out=x_grouped[:, :, :2].rearrange("p (c i) t -> p c t i", i=4), in_=x_early[:].rearrange("p t (c i) -> p c t i", i=4))
        for slots in halves:
            for v in range(2):
                nc.vector.tensor_copy(out=x_grouped[:, slots, 2 + v], in_=listed(xT_sb[1][:, v, :], slots))

        def quantise_x(slots):
            nc.vector.quantize_mx(
                out=x_codes[:, slots].bitcast(FP8X4), scales=x_scales[:, slots], in_=x_grouped[:, slots, :].rearrange("p c t -> p (c t)")
            )

        quantise_x(halves[0])

        pc_grouped = keep.tile([P, LANES, P, LANES], BF16, name="pc_grouped", tag="x_early", align_bytes=64)
        dealt = pc_grouped[:].rearrange("p t m j -> p m j t")
        source = pc_sb[:].rearrange("p j (m t) -> p m j t", t=LANES)
        nc.scalar.copy(out=dealt[:, :SCALAR_DEAL], in_=source[:, :SCALAR_DEAL])
        nc.vector.tensor_copy(out=dealt[:, SCALAR_DEAL:], in_=source[:, SCALAR_DEAL:])
        quantise_x(halves[1])
        pc_codes = keep.tile([P, SLOTS], U32, name="pc_codes", align_bytes=64)
        pc_scales = keep.tile([P, SLOTS], U8, name="pc_scales", align_bytes=64)
        for first, end in ((0, 1), (1, 2), (2, LANES)):
            cols = slice(first * P, end * P)
            nc.vector.quantize_mx(
                out=pc_codes[:, cols].bitcast(FP8X4), scales=pc_scales[:, cols], in_=pc_grouped[:, first:end].rearrange("p t m j -> p (t m j)")
            )

        k0 = [keep.tile([P, HALF], F32, name=f"k0{h}", tag=f"k0{h}") for h in range(2)]
        k1 = [keep.tile([P, HALF], F32, name=f"k1{h}", tag=f"k1{h}") for h in range(2)]
        k2 = keep.tile([P, SLOTS], F32, name="k2", tag="k2")
        k3 = keep.tile([P, SLOTS], F32, name="k3")
        pieces = (
            (0, halves[0], "k0", k0[0][:]),
            (0, halves[1], "spare1", k0[1][:]),
            (1, every, "k1", None),
            (2, every, "k0", k2[:]),
            (3, every, "k1", k3[:]),
        )
        for n, (t, slots, tag, target) in enumerate(pieces):
            k_bank = psum.tile([P, slots.stop - slots.start], F32, name=f"k_bank{n}", tag=tag)
            nc.tensor.matmul_mx(
                out=k_bank[:],
                lhsT=pc_codes[:, runs[t]].bitcast(FP8X4),
                lhsT_scale=pc_scales[:, runs[t]],
                rhs=x_codes[:, slots].bitcast(FP8X4),
                rhs_scale=x_scales[:, slots],
                start=True,
                stop=True,
            )
            if t == 1:
                for h in range(2):
                    nc.scalar.copy(out=k1[h][:], in_=k_bank[:, halves[h]])
            else:
                nc.scalar.copy(out=target, in_=k_bank[:])

        sums = [psum.tile([P, P], F32, name=f"sums{b}", tag=f"sums{b}") for b in range(RUNS)]
        for b in range(RUNS):
            nc.tensor.matmul(sums[b][:], identity[:], identity[:], start=True, stop=False, is_transpose=True)
        cuts = (
            tuple((halves[h], k0[h][:]) for h in range(2)),
            tuple((halves[h], k1[h][:]) for h in range(2)),
            ((every, k2[:]),),
            tuple((run, k3[:, run]) for run in runs),
        )
        for t in range(LANES):
            q = keep.tile([P, SLOTS], F32, name=f"q{t}")
            for slots, k_piece in cuts[t]:
                nc.vector.tensor_tensor(q[:, slots], listed(xE_sb[t][:], slots), k_piece, MULT)
            for b in range(RUNS):
                nc.tensor.matmul(sums[b][:], q[:, runs[b]], identity[:], start=False, stop=t == LANES - 1, is_transpose=True)

        factor = keep.tile([P, SLOTS], F32, name="factor", tag="factor")
        summed = keep.tile([P, RUNS, P], F32, name="summed")
        zeros = keep.tile([P, ADDED], F32, name="zeros", tag="zeros")
        nc.gpsimd.memset(zeros[:], 0.0)
        up0 = keep.tile([P, SLOTS], F32, name="up0", tag="up0")
        spreads = []
        k_er_early = []
        for b in range(2):
            denominator = keep.tile([P, 1], F32, name=f"denominator{b}", tag=f"early{b}")
            nc.scalar.activation(out=summed[:, b, :], in_=sums[b][:], func=COPY, accum_out=denominator[:])
            inverse = keep.tile([P, 1], F32, name=f"inverse{b}")
            nc.vector.reciprocal(out=inverse[:], in_=denominator[:])
            spread = psum.tile([P, P], F32, name=f"spread{b}", tag=f"k{b}")
            nc.tensor.transpose(spread[:], inverse[:].to_broadcast([P, P]), identity[:])
            spreads.append(spread)
            k_er_early.append(keep.tile([P, P + (1 - b) * ADDED], F32, name=f"k_er_early{b}", tag=f"early{b}"))
            nc.vector.tensor_tensor(k_er_early[b][:, :P], k0[0][:, runs[b]], er_listed[:, runs[b]], MULT)
        k2_er = k_er_early[0][:, P:]
        nc.vector.tensor_tensor(k2_er, k2[:, :ADDED], er_listed[:, :ADDED], MULT)
        k_er_late = keep.tile([P, HALF], F32, name="k_er_late", tag="k00")
        nc.gpsimd.tensor_tensor(k_er_late[:], k0[1][:], er_listed[:, halves[1]], MULT)
        up2_first = keep.tile([P, ADDED], F32, name="up2_first")
        nc.vector.tensor_tensor(up0[:, runs[0]], spreads[0][:], k_er_early[0][:, :P], MULT)
        nc.vector.tensor_tensor(up0[:, runs[1]], spreads[1][:], k_er_early[1][:, :P], MULT)
        late_denominator = keep.tile([P, 2], F32, name="late_denominator")
        for i in range(2):
            nc.scalar.activation(out=summed[:, 2 + i, :], in_=sums[2 + i][:], func=COPY, accum_out=late_denominator[:, i : i + 1])
        late_spread = psum.tile([P, 2, P], F32, name="late_spread", tag="spare1")
        late_inverse = keep.tile([P, 2], F32, name="late_inverse")
        nc.vector.reciprocal(out=late_inverse[:], in_=late_denominator[:])
        for i in range(2):
            nc.tensor.transpose(late_spread[:, i, :], late_inverse[:, i : i + 1].to_broadcast([P, P]), identity[:])
        late_flat = late_spread[:].rearrange("p i m -> p (i m)")
        for b in range(2):
            nc.vector.tensor_tensor(factor[:, runs[b]], spreads[b][:], er_listed[:, runs[b]], MULT)
        nc.vector.tensor_tensor(up2_first[:, :P], spreads[0][:], k2_er[:, :P], MULT)
        nc.vector.tensor_tensor(up2_first[:, P:], spreads[1][:, : ADDED - P], k2_er[:, P:], MULT)
        up1_early = keep.tile([P, HALF], F32, name="up1_early")
        nc.gpsimd.tensor_tensor(up1_early[:], k1[0][:], factor[:, halves[0]], MULT)
        nc.vector.tensor_tensor(factor[:, halves[1]], late_flat, er_listed[:, halves[1]], MULT)
        nc.vector.tensor_tensor(up0[:, halves[1]], late_flat, k_er_late[:], MULT)
        nc.vector.tensor_tensor(listed(windows[2][:], slice(0, ADDED)), up2_first[:], zeros[:], mybir.AluOpType.add)
        rest = slice(ADDED, SLOTS)
        up_late = keep.tile([P, 2, SLOTS], F32, name="up_late", tag="k00")
        nc.gpsimd.tensor_tensor(up_late[:, 1, halves[0]], k3[:, halves[0]], factor[:, halves[0]], MULT)
        up1_late = keep.tile([P, HALF], F32, name="up1_late", tag="zeros")
        nc.gpsimd.tensor_tensor(up1_late[:], k1[1][:], factor[:, halves[1]], MULT)
        nc.gpsimd.tensor_tensor(up_late[:, 0, rest], k2[:, rest], factor[:, rest], MULT)
        nc.gpsimd.tensor_tensor(up_late[:, 1, halves[1]], k3[:, halves[1]], factor[:, halves[1]], MULT)

        def scatter_on_scalar(t, slots, source):
            nc.scalar.activation(out=listed(windows[t][:], slots), in_=source, func=COPY)

        def store_lane(t):
            nc.sync.dma_start(out_rows[:, t, :], windows[t][:])

        vector_pairs = keep.tile([P, UNITS - SCALAR_UNITS, 2, UNIT, 2], BF16, name="vector_pairs", tag="k2")
        scalar_pairs = keep.tile([P, SCALAR_UNITS, 2, UNIT, 2], BF16, name="scalar_pairs", tag="zeros")

        def pairs(first, last):
            if first < SCALAR_UNITS:
                return scalar_pairs[:, first:last]
            return vector_pairs[:, first - SCALAR_UNITS : last - SCALAR_UNITS]

        def write_lane(engine, t, first, last):
            source = windows[t][:, first * UNIT : last * UNIT].rearrange("p (n h c) -> p h n c", h=2, c=UNIT // 2)
            target = pairs(first, last)[:, :, t // 2, :, t % 2].rearrange("p n (h c) -> p h n c", h=2)
            copy_on(nc, engine, target, source)

        scatter_on_scalar(0, halves[0], up0[:, halves[0]])
        scatter_on_scalar(1, halves[0], up1_early[:])
        for t, product in enumerate((up0[:, halves[1]], up1_late[:])):
            nc.vector.tensor_copy(out=listed(windows[t][:], halves[1]), in_=product)
            store_lane(t)
        scatter_on_scalar(3, halves[0], up_late[:, 1, halves[0]])
        scatter_on_scalar(2, rest, up_late[:, 0, rest])
        scatter_on_scalar(3, halves[1], up_late[:, 1, halves[1]])
        for t in (2, 3):
            store_lane(t)
        for t in range(3):
            write_lane("vector", t, SCALAR_UNITS, UNITS)
            if t < 2:
                write_lane("vector", t, 0, SCALAR_UNITS)
        for t in (2, 3):
            write_lane("scalar", t, 0, SCALAR_UNITS)

        words_out = out_1[0].rearrange("p c l -> p (c l)").bitcast(I32)
        out_scales = keep.tile([P, PLANE], U8, name="out_scales", align_bytes=64)
        grouped = keep.tile([P, TABLE * LANES], BF16, name="grouped", align_bytes=64)
        codes = keep.tile([P, TABLE], U32, name="codes", align_bytes=64)

        def merge(engine, first, last):
            word = U32 if engine == "scalar" else I32
            source = pairs(first, last).rearrange("p n u c v -> p n u (c v)").bitcast(word).rearrange("p n u (h c) -> p h n c u", h=2)
            target = grouped[:, first * UNIT * LANES : last * UNIT * LANES]
            copy_on(nc, engine, target.bitcast(word).rearrange("p (n h c u) -> p h n c u", h=2, c=UNIT // 2, u=2), source)

        def quantise(first, last):
            cols = slice(first * UNIT, last * UNIT)
            plane, start = divmod(first * UNIT, PLANE)
            nc.vector.quantize_mx(
                out=codes[:, cols].bitcast(FP8X4),
                scales=out_scales[4 * plane :, start : start + (last - first) * UNIT],
                in_=grouped[:, first * UNIT * LANES : last * UNIT * LANES],
            )

        def store(first, last):
            cols = slice(first * UNIT, last * UNIT)
            nc.sync.dma_start(words_out[:, cols], codes[:, cols].bitcast(I32))

        for first, last in ((3, 8), (8, 16)):
            write_lane("vector", 3, first, last)
        for first, last in ((0, 3), (3, 5), (8, 10), (10, 12), (12, 14), (14, 16)):
            merge("scalar", first, last)
        merge("vector", 5, 8)
        for first, last in ((0, 6), (6, 12), (12, 16)):
            for unit in range(first, last, 2):
                quantise(unit, unit + 2)
            store(first, last)
        scales_out = out_2[0].bitcast(I32).rearrange("r (j c) -> j r c", j=4)
        for quadrant in range(4):
            queue = nc.sync if quadrant % 2 == 0 else nc.scalar
            queue.dma_start(scales_out[:, 4 * quadrant : 4 * quadrant + 4, :], out_scales[32 * quadrant : 32 * quadrant + 16, :].bitcast(I32))
